import numpy as np
import ml_dtypes


def mxq(x, axis, fmt="e4m3"):
    dtype, down = {"e4m3": (ml_dtypes.float8_e4m3fn, 7), "e5m2": (ml_dtypes.float8_e5m2, 14)}[fmt]
    v = np.moveaxis(np.asarray(x, np.float32).astype(ml_dtypes.bfloat16).astype(np.float64), axis, -1)
    blocks = v.reshape(v.shape[:-1] + (-1, 32))
    amax = np.abs(blocks).max(-1, keepdims=True)
    byte = np.maximum(np.where(amax > 0, np.frexp(amax)[1] - 1 + 127, 0) - down, 1)
    scale = np.exp2(byte - 127.0)
    codes = (blocks / scale).astype(np.float32).astype(dtype).astype(np.float64)
    return np.moveaxis((codes * scale).reshape(v.shape), -1, axis)


WIDE = False


def mx_kscale(k):
    if not WIDE:
        return np.ones(k)
    levels = np.array([24, -24, 12, -12, 0])
    if k % 512:
        return np.exp2(np.random.permutation(np.resize(levels, k // 32))).repeat(32)
    a = np.empty((k // 512, 16))
    for p in range(k // 512):
        a[p, :8] = np.random.permutation(np.resize(levels, 8))
        for g in range(8):
            far = levels[np.abs(levels - a[p, g]) >= 10]
            a[p, g + 8] = far[np.random.randint(len(far))]
    return np.exp2(a.ravel()).repeat(32)


def f64(x):
    return np.asarray(x).astype(np.float64)


def striped(idx):
    return np.tile(idx.reshape(-1, 16).T, (8, 1)).astype(np.uint16)


def unstriped(offs):
    return offs[:16].T.reshape(-1).astype(np.int64)


E2M1 = np.array([0.0, 0.5, 1.0, 1.5, 2.0, 3.0, 4.0, 6.0, -0.0, -0.5, -1.0, -1.5, -2.0, -3.0, -4.0, -6.0])


def pack_weight(w, fmt):
    k, n = w.shape
    w = f64(np.asarray(w, np.float32).astype(ml_dtypes.bfloat16)).reshape(k // 32, 32, n)
    amax = np.abs(w).max(1)
    if fmt == "e4m3":
        byte = np.frexp(amax)[1] - 1 + 127 - 7
    else:
        mant, ex = np.frexp(amax / 6.0)
        byte = np.where(mant > 0.5, ex, ex - 1) + 127
    byte = np.clip(np.where(amax > 0, byte, 1), 1, 254)
    scaled = (w * np.exp2(127.0 - byte)[:, None, :]).reshape(k, n).astype(np.float32)
    by_word = np.ascontiguousarray(scaled.reshape(k // 512, 128, 4, n).transpose(0, 1, 3, 2))
    if fmt == "e4m3":
        words = by_word.astype(ml_dtypes.float8_e4m3fn).view(np.uint8)
    else:
        c = by_word.astype(ml_dtypes.float4_e2m1fn).view(np.uint8) & 0xF
        words = (c[..., 0::2] | (c[..., 1::2] << 4)).reshape(k // 512, 128, 2 * n)
    return np.ascontiguousarray(words), np.ascontiguousarray(byte.astype(np.uint8).reshape(k // 512, 16, n))


def unpack_weight(words, scales, fmt):
    g, _, n = scales.shape
    words = np.ascontiguousarray(words).reshape(g, 128, n, -1)
    if fmt == "e4m3":
        vals = words.view(ml_dtypes.float8_e4m3fn).astype(np.float64)
    else:
        nib = np.empty((g, 128, n, 4), np.uint8)
        nib[..., 0::2] = words & 0xF
        nib[..., 1::2] = words >> 4
        vals = E2M1[nib]
    vals = vals * np.repeat(np.exp2(scales.astype(np.float64) - 127.0), 8, axis=1)[..., None]
    return vals.transpose(0, 1, 3, 2).reshape(g * 512, n)


def pack_table4(v):
    words, scales = pack_weight(v, "e2m1")
    g, t = words.shape[0] // 2, v.shape[1]
    return np.ascontiguousarray(words.reshape(g, 2, 128, t, 2).transpose(0, 2, 3, 1, 4).reshape(g, 128, t, 4)), scales


def unpack_table4(words, scales):
    g, _, t, _ = words.shape
    return unpack_weight(words.reshape(g, 128, t, 2, 2).transpose(0, 3, 1, 2, 4).reshape(2 * g, 128, 2 * t), scales, "e2m1")


K, L, N, T, J = 1024, 512, 1024, 2048, 1024


def setup_inputs():
    n = np.random.standard_normal
    s = mx_kscale(K)[:, None]
    s2 = mx_kscale(L)[:, None]
    p_tab = pack_table4(n((K, T)) * s)
    p_wt = pack_weight(n((K, N)) / np.sqrt(K) / s, "e2m1")
    p_wx = pack_weight(n((L, N)) / np.sqrt(L) / s2, "e4m3")
    return {
        "tab_words": p_tab[0],
        "tab_scales": p_tab[1],
        "wt_words": p_wt[0],
        "wt_scales": p_wt[1],
        "x": (n((L, J)) * s2).astype(np.float32),
        "wx_words": p_wx[0],
        "wx_scales": p_wx[1],
        "offs": striped(np.random.permutation(T)[:J]),
    }


def reference(tab_words, tab_scales, wt_words, wt_scales, x, wx_words, wx_scales, offs):
    idx = unstriped(offs)
    tab_ = unpack_table4(tab_words, tab_scales)[:, idx]
    wt_ = unpack_weight(wt_words, wt_scales, "e2m1")
    x_q_ = mxq(f64(x), 0, "e4m3")
    x_r_ = mxq(f64(x) - x_q_, 0, "e4m3")
    wx_ = unpack_weight(wx_words, wx_scales, "e4m3")
    y = wt_.T @ tab_ + wx_.T @ x_q_ + wx_.T @ x_r_
    return y

@@ -1,0 +1,220 @@
+from contextlib import ExitStack
+
+import concourse.mybir as mybir
+
+K, L, N, T, J = 1024, 512, 1024, 2048, 1024
+FLOPS = 2 * N * J * (K + 2 * L)
+
+F32 = mybir.dt.float32
+BF16 = mybir.dt.bfloat16
+I32 = mybir.dt.int32
+U32 = mybir.dt.uint32
+U16 = mybir.dt.uint16
+U8 = mybir.dt.uint8
+FP8X4 = mybir.dt.float8_e4m3fn_x4
+FP4X4 = mybir.dt.float4_e2m1fn_x4
+
+P = 128
+PACK = 4
+BANK = 512
+CHUNKS = ((0, 256), (256, 256), (512, 512))
+PIECES = ((0, 128), (128, 128), (256, 256), (512, 256), (768, 256))
+
+
+def tile_list_tiert_none_kernel(
+    tc, tab_words, tab_scales, wt_words, wt_scales, x, wx_words, wx_scales, offs, out
+):
+    nc = tc.nc
+    with ExitStack() as ctx:
+        keep = ctx.enter_context(tc.tile_pool(name="keep", bufs=1))
+        stage = ctx.enter_context(tc.tile_pool(name="stage", bufs=8))
+        acc_pool = ctx.enter_context(tc.psum_pool(name="acc", bufs=6))
+        deq_pool = ctx.enter_context(tc.psum_pool(name="deq", bufs=2))
+
+        offsets = keep.tile([P, J // 16], U16, name="offsets")
+        diag = keep.tile([P, 520], BF16, name="diag", align_bytes=64)
+        tab_plane = keep.tile([P, T], U8, name="tab_plane", align_bytes=64)
+        wx_plane = keep.tile([P, N], U8, name="wx_plane", align_bytes=64)
+        wt_plane = keep.tile([P, 2 * N], U8, name="wt_plane", align_bytes=64)
+        tab = keep.tile([P, T], I32, name="tab", align_bytes=64)
+        wx = keep.tile([P, N], I32, name="wx", align_bytes=64)
+        wt = keep.tile([P, 2, 2 * N], U8, name="wt", align_bytes=64)
+        raw = [keep.tile([P, PACK, w], F32, name="raw%d" % j0, align_bytes=64) for j0, w in PIECES]
+        second = [keep.tile([P, w], U8, name="second%d" % j0, align_bytes=64) for j0, w in CHUNKS]
+
+        nc.vector.memset(diag[:].bitcast(I32), 0)
+        nc.vector.memset(tab_plane[:].bitcast(I32), 0)
+        nc.vector.memset(wx_plane[:].bitcast(I32), 0)
+        nc.vector.memset(wt_plane[:].bitcast(I32), 0)
+        for s in second:
+            nc.vector.memset(s[:].bitcast(I32), 0)
+
+        nc.gpsimd.affine_select(
+            out=diag[:], in_=diag[:], pattern=[[-1, 520]], compare_op=mybir.AluOpType.not_equal,
+            fill=1.0, base=3, channel_multiplier=4,
+        )
+
+        def load_x(i):
+            j0, w = PIECES[i]
+            nc.sync.dma_start(out=raw[i][:], in_=x[:, j0 : j0 + w].rearrange("(p t) j -> p t j", t=PACK))
+
+        load_x(0)
+        load_x(1)
+        nc.sync.dma_start(offsets[:], offs)
+        for q in range(4):
+            nc.sync.dma_start(
+                out=tab_plane[32 * q : 32 * q + 8, :].bitcast(I32),
+                in_=tab_scales[:, 4 * q : 4 * q + 4, :].bitcast(I32),
+            )
+        nc.sync.dma_start(out=wx[:], in_=wx_words[0].rearrange("p n b -> p (n b)").bitcast(I32))
+        for q in range(4):
+            nc.sync.dma_start(
+                out=wx_plane[32 * q : 32 * q + 4, :].bitcast(I32),
+                in_=wx_scales[0, 4 * q : 4 * q + 4, :].bitcast(I32),
+            )
+        nc.sync.dma_start(out=tab[:], in_=tab_words[0].rearrange("p t b -> p (t b)").bitcast(I32))
+        nc.sync.dma_start(out=wt[:].bitcast(I32), in_=wt_words.rearrange("a p c -> p a c").bitcast(I32))
+        for q in range(4):
+            nc.sync.dma_start(
+                out=wt_plane[32 * q : 32 * q + 4, :].rearrange("r (a n) -> r a n", a=2).bitcast(I32),
+                in_=wt_scales[:, 4 * q : 4 * q + 4, :].rearrange("a r n -> r a n").bitcast(I32),
+            )
+        for i in range(2, len(PIECES)):
+            load_x(i)
+
+        eye = keep.tile([P, PACK, BANK], BF16, name="eye", align_bytes=64)
+        for t in range(PACK):
+            nc.vector.tensor_copy(out=eye[:, t, :], in_=diag[:, 3 - t : 3 - t + BANK])
+        eye_codes = keep.tile([P, BANK], U32, name="eye_codes", align_bytes=64)
+        eye_plane = keep.tile([P, BANK], U8, name="eye_plane", align_bytes=64)
+        nc.vector.quantize_mx(
+            out=eye_codes[:].bitcast(FP8X4), scales=eye_plane[:], in_=eye[:].rearrange("p t c -> p (t c)")
+        )
+
+        tiers = {}
+        for j0, w in CHUNKS:
+            for tier in ("q", "r"):
+                tiers[(tier, j0)] = (
+                    keep.tile([P, w], U32, name="codes_%s%d" % (tier, j0), align_bytes=64),
+                    keep.tile([P, w], U8, name="plane_%s%d" % (tier, j0), align_bytes=64),
+                )
+
+        def woven(t):
+            return t.rearrange("p (c i t) -> p c t i", i=4, t=PACK)
+
+        def planar(t):
+            return t.rearrange("p t (c i) -> p c t i", i=4)
+
+        def two_tiers(i):
+            j0, w = PIECES[i]
+            c0 = max(c for c, cw in CHUNKS if c <= j0)
+            o = j0 - c0
+            q_codes, q_plane = tiers[("q", c0)]
+            r_codes, r_plane = tiers[("r", c0)]
+            rounded = keep.tile([P, PACK * w], BF16, name="rounded%d" % j0, align_bytes=64)
+            if i < 2:
+                nc.vector.tensor_copy(out=woven(rounded[:]), in_=planar(raw[i][:]))
+            else:
+                nc.scalar.copy(out=woven(rounded[:]), in_=planar(raw[i][:]))
+            nc.vector.quantize_mx(
+                out=q_codes[:, o : o + w].bitcast(FP8X4), scales=q_plane[:, o : o + w], in_=rounded[:]
+            )
+            left = keep.tile([P, PACK * w], BF16, name="left%d" % j0, align_bytes=64)
+            for s in range(0, w, P):
+                deq = deq_pool.tile([P, PACK, P], F32, name="deq")
+                for t in range(PACK):
+                    nc.tensor.matmul_mx(
+                        out=deq[:, t, :],
+                        lhsT=eye_codes[:, t * P : (t + 1) * P].bitcast(FP8X4),
+                        lhsT_scale=eye_plane[:, t * P : (t + 1) * P],
+                        rhs=q_codes[:, o + s : o + s + P].bitcast(FP8X4),
+                        rhs_scale=q_plane[:, o + s : o + s + P],
+                        start=True,
+                        stop=True,
+                    )
+                nc.vector.tensor_tensor(
+                    out=woven(left[:, PACK * s : PACK * (s + P)]),
+                    in0=planar(raw[i][:, :, s : s + P]),
+                    in1=planar(deq[:]),
+                    op=mybir.AluOpType.subtract,
+                )
+            nc.vector.quantize_mx(
+                out=r_codes[:, o : o + w].bitcast(FP8X4), scales=r_plane[:, o : o + w], in_=left[:]
+            )
+
+        picked = {}
+
+        def look_up(c):
+            j0, w = CHUNKS[c]
+            piece = offsets[:, j0 // 16 : (j0 + w) // 16]
+            first = keep.tile([P, w], U8, name="first%d" % j0, align_bytes=64)
+            nc.vector.tensor_copy(first[:], tab_plane[:].indirect(piece))
+            nc.sync.dma_start(out=second[c][0:112, :].bitcast(I32), in_=first[4:116, :].bitcast(I32))
+            pairs = keep.tile([P, w], U32, name="pairs%d" % j0, align_bytes=64)
+            nc.vector.tensor_copy(pairs[:], tab[:].bitcast(U32).indirect(piece))
+            parted = keep.tile([P, 2, 2 * w], U8, name="parted%d" % j0, align_bytes=64)
+            nc.vector.tensor_copy(
+                out=parted[:].bitcast(U16), in_=pairs[:].bitcast(U16).rearrange("p (j d) -> p d j", d=2)
+            )
+            picked[c] = (parted, (first, second[c]))
+
+        def multiply(c, order, by_pass):
+            j0, w = CHUNKS[c]
+            per_bank = BANK // w
+            n_banks = N // P // per_bank
+            parted, planes = picked[c]
+            banks = {}
+
+            def one(b, step):
+                if step == 0:
+                    banks[b] = acc_pool.tile([P, BANK], F32, name="acc")
+                for u in range(per_bank):
+                    n0 = (b * per_bank + u) * P
+                    kind = order[step]
+                    if kind in ("q", "r"):
+                        codes, plane = tiers[(kind, j0)]
+                        ops = dict(
+                            lhsT=wx[:, n0 : n0 + P].bitcast(FP8X4), lhsT_scale=wx_plane[:, n0 : n0 + P],
+                            rhs=codes[:].bitcast(FP8X4), rhs_scale=plane[:],
+                        )
+                    else:
+                        ops = dict(
+                            lhsT=wt[:, kind, 2 * n0 : 2 * (n0 + P)].bitcast(FP4X4),
+                            lhsT_scale=wt_plane[:, kind * N + n0 : kind * N + n0 + P],
+                            rhs=parted[:, kind, :].bitcast(FP4X4), rhs_scale=planes[kind][:],
+                        )
+                    nc.tensor.matmul_mx(
+                        out=banks[b][:, u * w : (u + 1) * w],
+                        start=(step == 0 and u == 0),
+                        stop=(step == 3 and u == per_bank - 1),
+                        **ops,
+                    )
+                if step == 3:
+                    result = stage.tile([P, BANK], F32, name="result")
+                    nc.scalar.copy(out=result[:], in_=banks[b][:])
+                    rows = out[b * per_bank * P : (b + 1) * per_bank * P, j0 : j0 + w]
+                    nc.sync.dma_start(
+                        out=rows.rearrange("(u p) j -> p u j", p=P),
+                        in_=result[:].rearrange("p (u j) -> p u j", u=per_bank),
+                    )
+
+            if by_pass:
+                for step in range(4):
+                    for b in range(n_banks):
+                        one(b, step)
+            else:
+                for b in range(n_banks):
+                    for step in range(4):
+                        one(b, step)
+
+        two_tiers(0)
+        two_tiers(1)
+        look_up(0)
+        look_up(1)
+        two_tiers(2)
+        multiply(0, ("q", "r", 0, 1), True)
+        two_tiers(3)
+        look_up(2)
+        two_tiers(4)
+        multiply(1, (0, 1, "q", "r"), False)
+        multiply(2, (0, 1, "q", "r"), False)

@@ -17,8 +17,9 @@ FP4X4 = mybir.dt.float4_e2m1fn_x4
 P = 128
 PACK = 4
 BANK = 512
-CHUNKS = ((0, 256), (256, 256), (512, 512))
-PIECES = ((0, 128), (128, 128), (256, 256), (512, 256), (768, 256))
+W = 256
+HALF = 128
+NEAR = 2
 
 
 def tile_list_tiert_none_kernel(
@@ -27,60 +28,50 @@ def tile_list_tiert_none_kernel(
     nc = tc.nc
     with ExitStack() as ctx:
         keep = ctx.enter_context(tc.tile_pool(name="keep", bufs=1))
+        lend = ctx.enter_context(tc.tile_pool(name="lend", bufs=1))
         stage = ctx.enter_context(tc.tile_pool(name="stage", bufs=8))
         acc_pool = ctx.enter_context(tc.psum_pool(name="acc", bufs=6))
         deq_pool = ctx.enter_context(tc.psum_pool(name="deq", bufs=2))
 
         offsets = keep.tile([P, J // 16], U16, name="offsets")
-        diag = keep.tile([P, 520], BF16, name="diag", align_bytes=64)
+        diag = lend.tile([P, 520], BF16, name="diag", align_bytes=64, offset=8192 + 512)
         tab_plane = keep.tile([P, T], U8, name="tab_plane", align_bytes=64)
         wx_plane = keep.tile([P, N], U8, name="wx_plane", align_bytes=64)
-        wt_plane = keep.tile([P, 2 * N], U8, name="wt_plane", align_bytes=64)
         tab = keep.tile([P, T], I32, name="tab", align_bytes=64)
         wx = keep.tile([P, N], I32, name="wx", align_bytes=64)
         wt = keep.tile([P, 2, 2 * N], U8, name="wt", align_bytes=64)
-        raw = [keep.tile([P, PACK, w], F32, name="raw%d" % j0, align_bytes=64) for j0, w in PIECES]
-        second = [keep.tile([P, w], U8, name="second%d" % j0, align_bytes=64) for j0, w in CHUNKS]
+        second = keep.tile([P, J], U8, name="second", align_bytes=64)
 
-        nc.vector.memset(diag[:].bitcast(I32), 0)
         nc.vector.memset(tab_plane[:].bitcast(I32), 0)
+        nc.vector.memset(diag[:].bitcast(I32), 0)
         nc.vector.memset(wx_plane[:].bitcast(I32), 0)
-        nc.vector.memset(wt_plane[:].bitcast(I32), 0)
-        for s in second:
-            nc.vector.memset(s[:].bitcast(I32), 0)
-
         nc.gpsimd.affine_select(
-            out=diag[:], in_=diag[:], pattern=[[-1, 520]], compare_op=mybir.AluOpType.not_equal,
-            fill=1.0, base=3, channel_multiplier=4,
+            out=diag[:].bitcast(F32), in_=diag[:].bitcast(F32), pattern=[[-1, 260]],
+            compare_op=mybir.AluOpType.not_equal, fill=1.0, base=1, channel_multiplier=2,
         )
 
-        def load_x(i):
-            j0, w = PIECES[i]
-            nc.sync.dma_start(out=raw[i][:], in_=x[:, j0 : j0 + w].rearrange("(p t) j -> p t j", t=PACK))
+        raw = {}
 
-        load_x(0)
-        load_x(1)
+        def load_x(j0, w, offset):
+            tile = lend.tile([P, PACK, w], F32, name="raw%d" % j0, align_bytes=64, offset=offset)
+            nc.sync.dma_start(out=tile[:], in_=x[:, j0 : j0 + w].rearrange("(p t) j -> p t j", t=PACK))
+            for s in range(0, w, HALF):
+                raw[j0 + s] = (tile, s)
+
         nc.sync.dma_start(offsets[:], offs)
+        load_x(0, W, 0)
+        nc.sync.dma_start(out=wx[:], in_=wx_words[0].rearrange("p n b -> p (n b)").bitcast(I32))
+        nc.sync.dma_start(out=tab[:], in_=tab_words[0].rearrange("p t b -> p (t b)").bitcast(I32))
         for q in range(4):
-            nc.sync.dma_start(
+            nc.scalar.dma_start(
                 out=tab_plane[32 * q : 32 * q + 8, :].bitcast(I32),
                 in_=tab_scales[:, 4 * q : 4 * q + 4, :].bitcast(I32),
             )
-        nc.sync.dma_start(out=wx[:], in_=wx_words[0].rearrange("p n b -> p (n b)").bitcast(I32))
         for q in range(4):
-            nc.sync.dma_start(
+            nc.scalar.dma_start(
                 out=wx_plane[32 * q : 32 * q + 4, :].bitcast(I32),
                 in_=wx_scales[0, 4 * q : 4 * q + 4, :].bitcast(I32),
             )
-        nc.sync.dma_start(out=tab[:], in_=tab_words[0].rearrange("p t b -> p (t b)").bitcast(I32))
-        nc.sync.dma_start(out=wt[:].bitcast(I32), in_=wt_words.rearrange("a p c -> p a c").bitcast(I32))
-        for q in range(4):
-            nc.sync.dma_start(
-                out=wt_plane[32 * q : 32 * q + 4, :].rearrange("r (a n) -> r a n", a=2).bitcast(I32),
-                in_=wt_scales[:, 4 * q : 4 * q + 4, :].rearrange("a r n -> r a n").bitcast(I32),
-            )
-        for i in range(2, len(PIECES)):
-            load_x(i)
 
         eye = keep.tile([P, PACK, BANK], BF16, name="eye", align_bytes=64)
         for t in range(PACK):
@@ -90,89 +81,95 @@ def tile_list_tiert_none_kernel(
         nc.vector.quantize_mx(
             out=eye_codes[:].bitcast(FP8X4), scales=eye_plane[:], in_=eye[:].rearrange("p t c -> p (t c)")
         )
+        wt_plane = keep.tile([P, 2 * N], U8, name="wt_plane", align_bytes=64)
+        nc.vector.memset(wt_plane[:].bitcast(I32), 0)
+        nc.vector.memset(second[:].bitcast(I32), 0)
+        for q in range(4):
+            nc.scalar.dma_start(
+                out=wt_plane[32 * q : 32 * q + 4, :].rearrange("r (a n) -> r a n", a=2).bitcast(I32),
+                in_=wt_scales[:, 4 * q : 4 * q + 4, :].rearrange("a r n -> r a n").bitcast(I32),
+            )
+        nc.sync.dma_start(out=wt[:].bitcast(I32), in_=wt_words.rearrange("a p c -> p a c").bitcast(I32))
 
         tiers = {}
-        for j0, w in CHUNKS:
+        for c in range(J // W):
             for tier in ("q", "r"):
-                tiers[(tier, j0)] = (
-                    keep.tile([P, w], U32, name="codes_%s%d" % (tier, j0), align_bytes=64),
-                    keep.tile([P, w], U8, name="plane_%s%d" % (tier, j0), align_bytes=64),
+                tiers[(tier, c)] = (
+                    keep.tile([P, W], U32, name="codes_%s%d" % (tier, c), align_bytes=64),
+                    keep.tile([P, W], U8, name="plane_%s%d" % (tier, c), align_bytes=64),
                 )
 
         def woven(t):
-            return t.rearrange("p (c i t) -> p c t i", i=4, t=PACK)
+            return t.rearrange("p (c i t) -> p c t i", i=NEAR, t=PACK)
 
         def planar(t):
-            return t.rearrange("p t (c i) -> p c t i", i=4)
+            return t.rearrange("p t (c i) -> p c t i", i=NEAR)
 
-        def two_tiers(i):
-            j0, w = PIECES[i]
-            c0 = max(c for c, cw in CHUNKS if c <= j0)
-            o = j0 - c0
-            q_codes, q_plane = tiers[("q", c0)]
-            r_codes, r_plane = tiers[("r", c0)]
-            rounded = keep.tile([P, PACK * w], BF16, name="rounded%d" % j0, align_bytes=64)
-            if i < 2:
-                nc.vector.tensor_copy(out=woven(rounded[:]), in_=planar(raw[i][:]))
-            else:
-                nc.scalar.copy(out=woven(rounded[:]), in_=planar(raw[i][:]))
-            nc.vector.quantize_mx(
-                out=q_codes[:, o : o + w].bitcast(FP8X4), scales=q_plane[:, o : o + w], in_=rounded[:]
-            )
-            left = keep.tile([P, PACK * w], BF16, name="left%d" % j0, align_bytes=64)
-            for s in range(0, w, P):
-                deq = deq_pool.tile([P, PACK, P], F32, name="deq")
-                for t in range(PACK):
-                    nc.tensor.matmul_mx(
-                        out=deq[:, t, :],
-                        lhsT=eye_codes[:, t * P : (t + 1) * P].bitcast(FP8X4),
-                        lhsT_scale=eye_plane[:, t * P : (t + 1) * P],
-                        rhs=q_codes[:, o + s : o + s + P].bitcast(FP8X4),
-                        rhs_scale=q_plane[:, o + s : o + s + P],
-                        start=True,
-                        stop=True,
-                    )
-                nc.vector.tensor_tensor(
-                    out=woven(left[:, PACK * s : PACK * (s + P)]),
-                    in0=planar(raw[i][:, :, s : s + P]),
-                    in1=planar(deq[:]),
-                    op=mybir.AluOpType.subtract,
+        def first_tier(j0, w, copy, rounded):
+            tile, s = raw[j0]
+            codes, plane = tiers[("q", j0 // W)]
+            o = j0 % W
+            copy(out=woven(rounded[:]), in_=planar(tile[:, :, s : s + w]))
+            nc.vector.quantize_mx(out=codes[:, o : o + w].bitcast(FP8X4), scales=plane[:, o : o + w], in_=rounded[:])
+
+        def left_over(j0, left):
+            tile, s = raw[j0]
+            c, o = divmod(j0, W)
+            codes, plane = tiers[("q", c)]
+            deq = deq_pool.tile([P, PACK, HALF], F32, name="deq")
+            for t in range(PACK):
+                nc.tensor.matmul_mx(
+                    out=deq[:, t, :],
+                    lhsT=eye_codes[:, t * P : (t + 1) * P].bitcast(FP8X4),
+                    lhsT_scale=eye_plane[:, t * P : (t + 1) * P],
+                    rhs=codes[:, o : o + HALF].bitcast(FP8X4),
+                    rhs_scale=plane[:, o : o + HALF],
+                    start=True,
+                    stop=True,
                 )
-            nc.vector.quantize_mx(
-                out=r_codes[:, o : o + w].bitcast(FP8X4), scales=r_plane[:, o : o + w], in_=left[:]
+            nc.vector.tensor_tensor(
+                out=woven(left[:, PACK * o : PACK * (o + HALF)]),
+                in0=planar(tile[:, :, s : s + HALF]),
+                in1=planar(deq[:]),
+                op=mybir.AluOpType.subtract,
             )
 
-        picked = {}
+        def second_tier(c, left):
+            codes, plane = tiers[("r", c)]
+            nc.vector.quantize_mx(out=codes[:].bitcast(FP8X4), scales=plane[:], in_=left[:])
 
-        def look_up(c):
-            j0, w = CHUNKS[c]
-            piece = offsets[:, j0 // 16 : (j0 + w) // 16]
-            first = keep.tile([P, w], U8, name="first%d" % j0, align_bytes=64)
-            nc.vector.tensor_copy(first[:], tab_plane[:].indirect(piece))
-            nc.sync.dma_start(out=second[c][0:112, :].bitcast(I32), in_=first[4:116, :].bitcast(I32))
-            pairs = keep.tile([P, w], U32, name="pairs%d" % j0, align_bytes=64)
-            nc.vector.tensor_copy(pairs[:], tab[:].bitcast(U32).indirect(piece))
-            parted = keep.tile([P, 2, 2 * w], U8, name="parted%d" % j0, align_bytes=64)
+        planes = {}
+
+        def look_up_scales(c0, c1, first):
+            nc.vector.tensor_copy(first[:], tab_plane[:].indirect(offsets[:, c0 * W // 16 : c1 * W // 16]))
+            for c in range(c0, c1):
+                planes[c] = (first[:, (c - c0) * W : (c - c0 + 1) * W], second[:, c * W : (c + 1) * W])
+
+        def shift_scales(c0, c1, first, queue):
+            queue.dma_start(out=second[0:112, c0 * W : c1 * W].bitcast(I32), in_=first[4:116, :].bitcast(I32))
+
+        parted = {}
+
+        def look_up_words(c, pairs):
+            nc.vector.tensor_copy(pairs[:], tab[:].bitcast(U32).indirect(offsets[:, c * W // 16 : (c + 1) * W // 16]))
+            parted[c] = keep.tile([P, 2, 2 * W], U8, name="parted%d" % c, align_bytes=64)
             nc.vector.tensor_copy(
-                out=parted[:].bitcast(U16), in_=pairs[:].bitcast(U16).rearrange("p (j d) -> p d j", d=2)
+                out=parted[c][:].bitcast(U16), in_=pairs[:].bitcast(U16).rearrange("p (j d) -> p d j", d=2)
             )
-            picked[c] = (parted, (first, second[c]))
 
-        def multiply(c, order, by_pass):
-            j0, w = CHUNKS[c]
-            per_bank = BANK // w
-            n_banks = N // P // per_bank
-            parted, planes = picked[c]
-            banks = {}
+        banks = {}
+        done = {}
 
-            def one(b, step):
-                if step == 0:
-                    banks[b] = acc_pool.tile([P, BANK], F32, name="acc")
-                for u in range(per_bank):
-                    n0 = (b * per_bank + u) * P
-                    kind = order[step]
+        def passes(c, tiles, kinds):
+            key = (c, tiles[0])
+            if key not in banks:
+                banks[key] = acc_pool.tile([P, BANK], F32, name="acc")
+                done[key] = 0
+            for kind in kinds:
+                for u, m in enumerate(tiles):
+                    n0 = m * P
                     if kind in ("q", "r"):
-                        codes, plane = tiers[(kind, j0)]
+                        codes, plane = tiers[(kind, c)]
                         ops = dict(
                             lhsT=wx[:, n0 : n0 + P].bitcast(FP8X4), lhsT_scale=wx_plane[:, n0 : n0 + P],
                             rhs=codes[:].bitcast(FP8X4), rhs_scale=plane[:],
@@ -181,40 +178,86 @@ def tile_list_tiert_none_kernel(
                         ops = dict(
                             lhsT=wt[:, kind, 2 * n0 : 2 * (n0 + P)].bitcast(FP4X4),
                             lhsT_scale=wt_plane[:, kind * N + n0 : kind * N + n0 + P],
-                            rhs=parted[:, kind, :].bitcast(FP4X4), rhs_scale=planes[kind][:],
+                            rhs=parted[c][:, kind, :].bitcast(FP4X4), rhs_scale=planes[c][kind],
                         )
                     nc.tensor.matmul_mx(
-                        out=banks[b][:, u * w : (u + 1) * w],
-                        start=(step == 0 and u == 0),
-                        stop=(step == 3 and u == per_bank - 1),
+                        out=banks[key][:, u * W : (u + 1) * W],
+                        start=(done[key] == 0),
+                        stop=(done[key] == 4 * len(tiles) - 1),
                         **ops,
                     )
-                if step == 3:
-                    result = stage.tile([P, BANK], F32, name="result")
-                    nc.scalar.copy(out=result[:], in_=banks[b][:])
-                    rows = out[b * per_bank * P : (b + 1) * per_bank * P, j0 : j0 + w]
-                    nc.sync.dma_start(
-                        out=rows.rearrange("(u p) j -> p u j", p=P),
-                        in_=result[:].rearrange("p (u j) -> p u j", u=per_bank),
-                    )
+                    done[key] = done[key] + 1
+            if done[key] == 4 * len(tiles):
+                width = len(tiles) * W
+                result = stage.tile([P, width], F32, name="result")
+                nc.scalar.copy(out=result[:], in_=banks[key][:, 0:width])
+                rows = out[tiles[0] * P : (tiles[-1] + 1) * P, c * W : (c + 1) * W]
+                nc.sync.dma_start(
+                    out=rows.rearrange("(u p) j -> p u j", p=P),
+                    in_=result[:].rearrange("p (u j) -> p u j", u=len(tiles)),
+                )
 
-            if by_pass:
-                for step in range(4):
-                    for b in range(n_banks):
-                        one(b, step)
-            else:
-                for b in range(n_banks):
-                    for step in range(4):
-                        one(b, step)
+        def own(shape, dtype, name):
+            return keep.tile(shape, dtype, name=name, align_bytes=64)
 
-        two_tiers(0)
-        two_tiers(1)
-        look_up(0)
-        look_up(1)
-        two_tiers(2)
-        multiply(0, ("q", "r", 0, 1), True)
-        two_tiers(3)
-        look_up(2)
-        two_tiers(4)
-        multiply(1, (0, 1, "q", "r"), False)
-        multiply(2, (0, 1, "q", "r"), False)
+        def lent(shape, dtype, name, offset):
+            return lend.tile(shape, dtype, name=name, align_bytes=64, offset=offset)
+
+        pairs_of_tiles = [(m, m + 1) for m in range(0, N // P, 2)]
+
+        load_x(W, W, 12288)
+        left0 = lent([P, PACK * W], BF16, "left0", 20480)
+        for s in (0, HALF):
+            first_tier(s, HALF, nc.vector.tensor_copy, lent([P, PACK * HALF], BF16, "rounded%d" % s, 8192 + 8 * s))
+        first0 = lent([P, W], U8, "first0", 8192)
+        look_up_scales(0, 1, first0)
+        shift_scales(0, 1, first0, nc.scalar)
+        for s in (0, HALF):
+            left_over(s, left0)
+        first1 = lent([P, W], U8, "first1", 0)
+        look_up_scales(1, 2, first1)
+        second_tier(0, left0)
+        load_x(2 * W, W, 3840)
+        shift_scales(1, 2, first1, nc.sync)
+        load_x(3 * W, W, 20480)
+        for tier in ("q", "r"):
+            for tiles in pairs_of_tiles:
+                passes(0, tiles, (tier,))
+
+        look_up_words(0, lent([P, W], U32, "pairs0", 1280))
+        look_up_words(1, lent([P, W], U32, "pairs1", 768))
+        first23 = lent([P, 2 * W], U8, "first23", 768)
+        look_up_scales(2, 4, first23)
+        shift_scales(2, 4, first23, nc.sync)
+        first_tier(W, W, nc.scalar.copy, lent([P, PACK * W], BF16, "rounded256", 1792))
+        look_up_words(2, lent([P, W], U32, "pairs2", 1792))
+        first_tier(2 * W, W, nc.scalar.copy, lent([P, PACK * W], BF16, "rounded512", 16384))
+        for a in range(2):
+            for tiles in pairs_of_tiles:
+                passes(0, tiles, (a,))
+            for tiles in pairs_of_tiles[:2]:
+                passes(1, tiles, (a,))
+        left1 = lent([P, PACK * W], BF16, "left1", 24576)
+        left_over(W, left1)
+        left_over(W + HALF, left1)
+        second_tier(1, left1)
+        for tiles in pairs_of_tiles[2:]:
+            passes(1, tiles, (0, 1))
+        left2 = own([P, PACK * W], BF16, "left2")
+        left_over(2 * W, left2)
+        left_over(2 * W + HALF, left2)
+        second_tier(2, left2)
+        look_up_words(3, lent([P, W], U32, "pairs3", 24576))
+        first_tier(3 * W, W, nc.scalar.copy, lent([P, PACK * W], BF16, "rounded768", 17408))
+        for tiles in pairs_of_tiles:
+            passes(1, tiles, ("q", "r"))
+        for tiles in pairs_of_tiles[:2]:
+            passes(2, tiles, (0, 1, "q", "r"))
+        left3 = own([P, PACK * W], BF16, "left3")
+        left_over(3 * W, left3)
+        left_over(3 * W + HALF, left3)
+        second_tier(3, left3)
+        for tiles in pairs_of_tiles[2:]:
+            passes(2, tiles, (0, 1, "q", "r"))
+        for tiles in pairs_of_tiles[:3] + [(6,), (7,)]:
+            passes(3, tiles, (0, 1, "q", "r"))

@@ -42,9 +42,13 @@ def tile_list_tiert_none_kernel(
         wt = keep.tile([P, 2, 2 * N], U8, name="wt", align_bytes=64)
         second = keep.tile([P, J], U8, name="second", align_bytes=64)
 
+        wt_plane = keep.tile([P, 2 * N], U8, name="wt_plane", align_bytes=64)
         nc.vector.memset(tab_plane[:].bitcast(I32), 0)
-        nc.vector.memset(diag[:].bitcast(I32), 0)
         nc.vector.memset(wx_plane[:].bitcast(I32), 0)
+        nc.vector.memset(wt_plane[:].bitcast(I32), 0)
+        nc.vector.memset(second[:].bitcast(I32), 0)
+
+        nc.gpsimd.memset(diag[:].bitcast(F32), 0.0)
         nc.gpsimd.affine_select(
             out=diag[:].bitcast(F32), in_=diag[:].bitcast(F32), pattern=[[-1, 260]],
             compare_op=mybir.AluOpType.not_equal, fill=1.0, base=1, channel_multiplier=2,
@@ -58,20 +62,26 @@ def tile_list_tiert_none_kernel(
             for s in range(0, w, HALF):
                 raw[j0 + s] = (tile, s)
 
-        nc.sync.dma_start(offsets[:], offs)
         load_x(0, W, 0)
-        nc.sync.dma_start(out=wx[:], in_=wx_words[0].rearrange("p n b -> p (n b)").bitcast(I32))
-        nc.sync.dma_start(out=tab[:], in_=tab_words[0].rearrange("p t b -> p (t b)").bitcast(I32))
-        for q in range(4):
-            nc.scalar.dma_start(
-                out=tab_plane[32 * q : 32 * q + 8, :].bitcast(I32),
-                in_=tab_scales[:, 4 * q : 4 * q + 4, :].bitcast(I32),
+        nc.sync.dma_start(offsets[:], offs)
+        for r in range(4):
+            nc.sync.dma_start(
+                out=tab_plane[r:P:16, :].bitcast(I32),
+                in_=tab_scales.rearrange("a (q r) t -> r q a t", r=4)[r].bitcast(I32),
             )
+        nc.sync.dma_start(out=wx[:], in_=wx_words[0].rearrange("p n b -> p (n b)").bitcast(I32))
         for q in range(4):
-            nc.scalar.dma_start(
+            nc.sync.dma_start(
                 out=wx_plane[32 * q : 32 * q + 4, :].bitcast(I32),
                 in_=wx_scales[0, 4 * q : 4 * q + 4, :].bitcast(I32),
             )
+        nc.sync.dma_start(out=tab[:], in_=tab_words[0].rearrange("p t b -> p (t b)").bitcast(I32))
+        for q in range(4):
+            nc.sync.dma_start(
+                out=wt_plane[32 * q : 32 * q + 4, :].rearrange("r (a n) -> r a n", a=2).bitcast(I32),
+                in_=wt_scales[:, 4 * q : 4 * q + 4, :].rearrange("a r n -> r a n").bitcast(I32),
+            )
+        nc.sync.dma_start(out=wt[:].bitcast(I32), in_=wt_words.rearrange("a p c -> p a c").bitcast(I32))
 
         eye = keep.tile([P, PACK, BANK], BF16, name="eye", align_bytes=64)
         for t in range(PACK):
@@ -81,21 +91,13 @@ def tile_list_tiert_none_kernel(
         nc.vector.quantize_mx(
             out=eye_codes[:].bitcast(FP8X4), scales=eye_plane[:], in_=eye[:].rearrange("p t c -> p (t c)")
         )
-        wt_plane = keep.tile([P, 2 * N], U8, name="wt_plane", align_bytes=64)
-        nc.vector.memset(wt_plane[:].bitcast(I32), 0)
-        nc.vector.memset(second[:].bitcast(I32), 0)
-        for q in range(4):
-            nc.scalar.dma_start(
-                out=wt_plane[32 * q : 32 * q + 4, :].rearrange("r (a n) -> r a n", a=2).bitcast(I32),
-                in_=wt_scales[:, 4 * q : 4 * q + 4, :].rearrange("a r n -> r a n").bitcast(I32),
-            )
-        nc.sync.dma_start(out=wt[:].bitcast(I32), in_=wt_words.rearrange("a p c -> p a c").bitcast(I32))
-
         tiers = {}
         for c in range(J // W):
             for tier in ("q", "r"):
                 tiers[(tier, c)] = (
-                    keep.tile([P, W], U32, name="codes_%s%d" % (tier, c), align_bytes=64),
+                    lend.tile([P, W], U32, name="codes_q0", align_bytes=64, offset=8192 + 1024)
+                    if (tier, c) == ("q", 0)
+                    else keep.tile([P, W], U32, name="codes_%s%d" % (tier, c), align_bytes=64),
                     keep.tile([P, W], U8, name="plane_%s%d" % (tier, c), align_bytes=64),
                 )
 
@@ -105,11 +107,14 @@ def tile_list_tiert_none_kernel(
         def planar(t):
             return t.rearrange("p t (c i) -> p c t i", i=NEAR)
 
-        def first_tier(j0, w, copy, rounded):
+        def round_x(j0, w, copy, rounded):
             tile, s = raw[j0]
+            copy(out=woven(rounded[:]), in_=planar(tile[:, :, s : s + w]))
+            return rounded
+
+        def first_tier(j0, w, rounded):
             codes, plane = tiers[("q", j0 // W)]
             o = j0 % W
-            copy(out=woven(rounded[:]), in_=planar(tile[:, :, s : s + w]))
             nc.vector.quantize_mx(out=codes[:, o : o + w].bitcast(FP8X4), scales=plane[:, o : o + w], in_=rounded[:])
 
         def left_over(j0, left):
@@ -146,7 +151,7 @@ def tile_list_tiert_none_kernel(
                 planes[c] = (first[:, (c - c0) * W : (c - c0 + 1) * W], second[:, c * W : (c + 1) * W])
 
         def shift_scales(c0, c1, first, queue):
-            queue.dma_start(out=second[0:112, c0 * W : c1 * W].bitcast(I32), in_=first[4:116, :].bitcast(I32))
+            queue.dma_start(out=second[0:112, c0 * W : c1 * W].bitcast(I32), in_=first[16:P, :].bitcast(I32))
 
         parted = {}
 
@@ -207,12 +212,14 @@ def tile_list_tiert_none_kernel(
 
         load_x(W, W, 12288)
         left0 = lent([P, PACK * W], BF16, "left0", 20480)
-        for s in (0, HALF):
-            first_tier(s, HALF, nc.vector.tensor_copy, lent([P, PACK * HALF], BF16, "rounded%d" % s, 8192 + 8 * s))
-        first0 = lent([P, W], U8, "first0", 8192)
+        low = round_x(0, HALF, nc.vector.tensor_copy, lent([P, PACK * HALF], BF16, "rounded0", 8192))
+        high = round_x(HALF, HALF, nc.scalar.copy, lent([P, PACK * HALF], BF16, "rounded128", 28672))
+        first_tier(HALF, HALF, high)
+        first_tier(0, HALF, low)
+        first0 = lent([P, W], U8, "first0", 28672)
         look_up_scales(0, 1, first0)
         shift_scales(0, 1, first0, nc.scalar)
-        for s in (0, HALF):
+        for s in (HALF, 0):
             left_over(s, left0)
         first1 = lent([P, W], U8, "first1", 0)
         look_up_scales(1, 2, first1)
@@ -229,9 +236,9 @@ def tile_list_tiert_none_kernel(
         first23 = lent([P, 2 * W], U8, "first23", 768)
         look_up_scales(2, 4, first23)
         shift_scales(2, 4, first23, nc.sync)
-        first_tier(W, W, nc.scalar.copy, lent([P, PACK * W], BF16, "rounded256", 1792))
+        first_tier(W, W, round_x(W, W, nc.scalar.copy, lent([P, PACK * W], BF16, "rounded256", 1792)))
         look_up_words(2, lent([P, W], U32, "pairs2", 1792))
-        first_tier(2 * W, W, nc.scalar.copy, lent([P, PACK * W], BF16, "rounded512", 16384))
+        first_tier(2 * W, W, round_x(2 * W, W, nc.scalar.copy, lent([P, PACK * W], BF16, "rounded512", 16384)))
         for a in range(2):
             for tiles in pairs_of_tiles:
                 passes(0, tiles, (a,))
@@ -248,7 +255,7 @@ def tile_list_tiert_none_kernel(
         left_over(2 * W + HALF, left2)
         second_tier(2, left2)
         look_up_words(3, lent([P, W], U32, "pairs3", 24576))
-        first_tier(3 * W, W, nc.scalar.copy, lent([P, PACK * W], BF16, "rounded768", 17408))
+        first_tier(3 * W, W, round_x(3 * W, W, nc.scalar.copy, lent([P, PACK * W], BF16, "rounded768", 17408)))
         for tiles in pairs_of_tiles:
             passes(1, tiles, ("q", "r"))
         for tiles in pairs_of_tiles[:2]:

@@ -39,7 +39,7 @@ def tile_list_tiert_none_kernel(
         wx_plane = keep.tile([P, N], U8, name="wx_plane", align_bytes=64)
         tab = keep.tile([P, T], I32, name="tab", align_bytes=64)
         wx = keep.tile([P, N], I32, name="wx", align_bytes=64)
-        wt = keep.tile([P, 2, 2 * N], U8, name="wt", align_bytes=64)
+        wt = [keep.tile([P, 2 * N], U8, name="wt%d" % a, align_bytes=64) for a in range(2)]
         second = keep.tile([P, J], U8, name="second", align_bytes=64)
 
         wt_plane = keep.tile([P, 2 * N], U8, name="wt_plane", align_bytes=64)
@@ -70,18 +70,19 @@ def tile_list_tiert_none_kernel(
                 in_=tab_scales.rearrange("a (q r) t -> r q a t", r=4)[r].bitcast(I32),
             )
         nc.sync.dma_start(out=wx[:], in_=wx_words[0].rearrange("p n b -> p (n b)").bitcast(I32))
-        for q in range(4):
+        for r in range(4):
             nc.sync.dma_start(
-                out=wx_plane[32 * q : 32 * q + 4, :].bitcast(I32),
-                in_=wx_scales[0, 4 * q : 4 * q + 4, :].bitcast(I32),
+                out=wx_plane[r:P:32, :].bitcast(I32),
+                in_=wx_scales[0].rearrange("(q r) n -> r q n", r=4)[r].bitcast(I32),
             )
         nc.sync.dma_start(out=tab[:], in_=tab_words[0].rearrange("p t b -> p (t b)").bitcast(I32))
-        for q in range(4):
+        for r in range(4):
             nc.sync.dma_start(
-                out=wt_plane[32 * q : 32 * q + 4, :].rearrange("r (a n) -> r a n", a=2).bitcast(I32),
-                in_=wt_scales[:, 4 * q : 4 * q + 4, :].rearrange("a r n -> r a n").bitcast(I32),
+                out=wt_plane[r:P:32, :].rearrange("q (a n) -> q a n", a=2).bitcast(I32),
+                in_=wt_scales.rearrange("a (q r) n -> r q a n", r=4)[r].bitcast(I32),
             )
-        nc.sync.dma_start(out=wt[:].bitcast(I32), in_=wt_words.rearrange("a p c -> p a c").bitcast(I32))
+        for a in range(2):
+            nc.sync.dma_start(out=wt[a][:].bitcast(I32), in_=wt_words[a].bitcast(I32))
 
         eye = keep.tile([P, PACK, BANK], BF16, name="eye", align_bytes=64)
         for t in range(PACK):
@@ -158,9 +159,12 @@ def tile_list_tiert_none_kernel(
         def look_up_words(c, pairs):
             nc.vector.tensor_copy(pairs[:], tab[:].bitcast(U32).indirect(offsets[:, c * W // 16 : (c + 1) * W // 16]))
             parted[c] = keep.tile([P, 2, 2 * W], U8, name="parted%d" % c, align_bytes=64)
-            nc.vector.tensor_copy(
-                out=parted[c][:].bitcast(U16), in_=pairs[:].bitcast(U16).rearrange("p (j d) -> p d j", d=2)
-            )
+            halves = pairs[:].bitcast(U16).rearrange("p (j d) -> p d j", d=2)
+            if c == 0:
+                for a in range(2):
+                    nc.vector.tensor_copy(out=parted[c][:, a, :].bitcast(U16), in_=halves[:, a, :])
+            else:
+                nc.vector.tensor_copy(out=parted[c][:].bitcast(U16), in_=halves)
 
         banks = {}
         done = {}
@@ -181,7 +185,7 @@ def tile_list_tiert_none_kernel(
                         )
                     else:
                         ops = dict(
-                            lhsT=wt[:, kind, 2 * n0 : 2 * (n0 + P)].bitcast(FP4X4),
+                            lhsT=wt[kind][:, 2 * n0 : 2 * (n0 + P)].bitcast(FP4X4),
                             lhsT_scale=wt_plane[:, kind * N + n0 : kind * N + n0 + P],
                             rhs=parted[c][:, kind, :].bitcast(FP4X4), rhs_scale=planes[c][kind],
                         )
@@ -210,44 +214,41 @@ def tile_list_tiert_none_kernel(
 
         pairs_of_tiles = [(m, m + 1) for m in range(0, N // P, 2)]
 
-        load_x(W, W, 12288)
         left0 = lent([P, PACK * W], BF16, "left0", 20480)
         low = round_x(0, HALF, nc.vector.tensor_copy, lent([P, PACK * HALF], BF16, "rounded0", 8192))
         high = round_x(HALF, HALF, nc.scalar.copy, lent([P, PACK * HALF], BF16, "rounded128", 28672))
         first_tier(HALF, HALF, high)
         first_tier(0, HALF, low)
-        first0 = lent([P, W], U8, "first0", 28672)
-        look_up_scales(0, 1, first0)
-        shift_scales(0, 1, first0, nc.scalar)
+        first01 = lent([P, 2 * W], U8, "first01", 28672)
+        look_up_scales(0, 2, first01)
+        shift_scales(0, 2, first01, nc.sync)
+        load_x(W, W, 12288)
         for s in (HALF, 0):
             left_over(s, left0)
-        first1 = lent([P, W], U8, "first1", 0)
-        look_up_scales(1, 2, first1)
         second_tier(0, left0)
-        load_x(2 * W, W, 3840)
-        shift_scales(1, 2, first1, nc.sync)
-        load_x(3 * W, W, 20480)
+        load_x(2 * W, W, 32768)
+        load_x(3 * W, W, 36864)
         for tier in ("q", "r"):
             for tiles in pairs_of_tiles:
                 passes(0, tiles, (tier,))
 
-        look_up_words(0, lent([P, W], U32, "pairs0", 1280))
-        look_up_words(1, lent([P, W], U32, "pairs1", 768))
-        first23 = lent([P, 2 * W], U8, "first23", 768)
+        look_up_words(0, lent([P, W], U32, "pairs0", 21504))
+        look_up_words(1, lent([P, W], U32, "pairs1", 21504))
+        first23 = lent([P, 2 * W], U8, "first23", 21504)
         look_up_scales(2, 4, first23)
         shift_scales(2, 4, first23, nc.sync)
-        first_tier(W, W, round_x(W, W, nc.scalar.copy, lent([P, PACK * W], BF16, "rounded256", 1792)))
-        look_up_words(2, lent([P, W], U32, "pairs2", 1792))
-        first_tier(2 * W, W, round_x(2 * W, W, nc.scalar.copy, lent([P, PACK * W], BF16, "rounded512", 16384)))
+        first_tier(W, W, round_x(W, W, nc.vector.tensor_copy, lent([P, PACK * W], BF16, "rounded256", 22016)))
         for a in range(2):
             for tiles in pairs_of_tiles:
                 passes(0, tiles, (a,))
-            for tiles in pairs_of_tiles[:2]:
-                passes(1, tiles, (a,))
+        for tiles in pairs_of_tiles[:2]:
+            passes(1, tiles, (1, 0))
         left1 = lent([P, PACK * W], BF16, "left1", 24576)
         left_over(W, left1)
         left_over(W + HALF, left1)
         second_tier(1, left1)
+        look_up_words(2, lent([P, W], U32, "pairs2", 22016))
+        first_tier(2 * W, W, round_x(2 * W, W, nc.scalar.copy, lent([P, PACK * W], BF16, "rounded512", 16384)))
         for tiles in pairs_of_tiles[2:]:
             passes(1, tiles, (0, 1))
         left2 = own([P, PACK * W], BF16, "left2")

@@ -156,8 +156,10 @@ def tile_list_tiert_none_kernel(
 
         parted = {}
 
-        def look_up_words(c, pairs):
+        def look_up_words(c, pairs, between):
             nc.vector.tensor_copy(pairs[:], tab[:].bitcast(U32).indirect(offsets[:, c * W // 16 : (c + 1) * W // 16]))
+            if between is not None:
+                between()
             parted[c] = keep.tile([P, 2, 2 * W], U8, name="parted%d" % c, align_bytes=64)
             halves = pairs[:].bitcast(U16).rearrange("p (j d) -> p d j", d=2)
             if c == 0:
@@ -232,12 +234,11 @@ def tile_list_tiert_none_kernel(
             for tiles in pairs_of_tiles:
                 passes(0, tiles, (tier,))
 
-        look_up_words(0, lent([P, W], U32, "pairs0", 21504))
-        look_up_words(1, lent([P, W], U32, "pairs1", 21504))
+        look_up_words(0, lent([P, W], U32, "pairs0", 21504), None)
         first23 = lent([P, 2 * W], U8, "first23", 21504)
-        look_up_scales(2, 4, first23)
+        look_up_words(1, lent([P, W], U32, "pairs1", 22016), lambda: look_up_scales(2, 4, first23))
         shift_scales(2, 4, first23, nc.sync)
-        first_tier(W, W, round_x(W, W, nc.vector.tensor_copy, lent([P, PACK * W], BF16, "rounded256", 22016)))
+        first_tier(W, W, round_x(W, W, nc.vector.tensor_copy, lent([P, PACK * W], BF16, "rounded256", 40960)))
         for a in range(2):
             for tiles in pairs_of_tiles:
                 passes(0, tiles, (a,))
@@ -247,7 +248,7 @@ def tile_list_tiert_none_kernel(
         left_over(W, left1)
         left_over(W + HALF, left1)
         second_tier(1, left1)
-        look_up_words(2, lent([P, W], U32, "pairs2", 22016))
+        look_up_words(2, lent([P, W], U32, "pairs2", 40960), None)
         first_tier(2 * W, W, round_x(2 * W, W, nc.scalar.copy, lent([P, PACK * W], BF16, "rounded512", 16384)))
         for tiles in pairs_of_tiles[2:]:
             passes(1, tiles, (0, 1))
@@ -255,7 +256,7 @@ def tile_list_tiert_none_kernel(
         left_over(2 * W, left2)
         left_over(2 * W + HALF, left2)
         second_tier(2, left2)
-        look_up_words(3, lent([P, W], U32, "pairs3", 24576))
+        look_up_words(3, lent([P, W], U32, "pairs3", 24576), None)
         first_tier(3 * W, W, round_x(3 * W, W, nc.scalar.copy, lent([P, PACK * W], BF16, "rounded768", 17408)))
         for tiles in pairs_of_tiles:
             passes(1, tiles, ("q", "r"))

@@ -19,6 +19,7 @@ PACK = 4
 BANK = 512
 W = 256
 HALF = 128
+QUARTER = 64
 NEAR = 2
 
 
@@ -34,7 +35,7 @@ def tile_list_tiert_none_kernel(
         deq_pool = ctx.enter_context(tc.psum_pool(name="deq", bufs=2))
 
         offsets = keep.tile([P, J // 16], U16, name="offsets")
-        diag = lend.tile([P, 520], BF16, name="diag", align_bytes=64, offset=8192 + 512)
+        diag = lend.tile([P, 520], BF16, name="diag", align_bytes=64, offset=8192 + 448)
         tab_plane = keep.tile([P, T], U8, name="tab_plane", align_bytes=64)
         wx_plane = keep.tile([P, N], U8, name="wx_plane", align_bytes=64)
         tab = keep.tile([P, T], I32, name="tab", align_bytes=64)
@@ -59,30 +60,53 @@ def tile_list_tiert_none_kernel(
         def load_x(j0, w, offset):
             tile = lend.tile([P, PACK, w], F32, name="raw%d" % j0, align_bytes=64, offset=offset)
             nc.sync.dma_start(out=tile[:], in_=x[:, j0 : j0 + w].rearrange("(p t) j -> p t j", t=PACK))
-            for s in range(0, w, HALF):
+            for s in range(0, w, QUARTER):
                 raw[j0 + s] = (tile, s)
 
-        load_x(0, W, 0)
-        nc.sync.dma_start(offsets[:], offs)
-        for r in range(4):
-            nc.sync.dma_start(
+        def load_tab_scales(r, queue):
+            queue.dma_start(
                 out=tab_plane[r:P:16, :].bitcast(I32),
                 in_=tab_scales.rearrange("a (q r) t -> r q a t", r=4)[r].bitcast(I32),
             )
-        nc.sync.dma_start(out=wx[:], in_=wx_words[0].rearrange("p n b -> p (n b)").bitcast(I32))
-        for r in range(4):
-            nc.sync.dma_start(
+
+        def load_wx_scales(r, queue):
+            queue.dma_start(
                 out=wx_plane[r:P:32, :].bitcast(I32),
                 in_=wx_scales[0].rearrange("(q r) n -> r q n", r=4)[r].bitcast(I32),
             )
-        nc.sync.dma_start(out=tab[:], in_=tab_words[0].rearrange("p t b -> p (t b)").bitcast(I32))
-        for r in range(4):
-            nc.sync.dma_start(
+
+        def load_wt_scales(r, queue):
+            queue.dma_start(
                 out=wt_plane[r:P:32, :].rearrange("q (a n) -> q a n", a=2).bitcast(I32),
                 in_=wt_scales.rearrange("a (q r) n -> r q a n", r=4)[r].bitcast(I32),
             )
-        for a in range(2):
+
+        def load_tab(h):
+            cols = slice(h * T // 2, (h + 1) * T // 2)
+            nc.sync.dma_start(out=tab[:, cols], in_=tab_words[0, :, cols, :].rearrange("p t b -> p (t b)").bitcast(I32))
+
+        def load_wt(a):
             nc.sync.dma_start(out=wt[a][:].bitcast(I32), in_=wt_words[a].bitcast(I32))
+
+        load_x(0, W, 0)
+        nc.sync.dma_start(offsets[:], offs)
+        load_tab_scales(0, nc.sync)
+        load_tab_scales(1, nc.sync)
+        load_tab_scales(2, nc.sync)
+        load_tab_scales(3, nc.sync)
+        nc.sync.dma_start(out=wx[:], in_=wx_words[0].rearrange("p n b -> p (n b)").bitcast(I32))
+        load_tab(0)
+        load_wx_scales(0, nc.sync)
+        load_wx_scales(1, nc.sync)
+        load_wx_scales(2, nc.sync)
+        load_wx_scales(3, nc.sync)
+        load_tab(1)
+        load_wt(0)
+        load_wt_scales(0, nc.sync)
+        load_wt_scales(1, nc.sync)
+        load_wt_scales(2, nc.sync)
+        load_wt_scales(3, nc.sync)
+        load_wt(1)
 
         eye = keep.tile([P, PACK, BANK], BF16, name="eye", align_bytes=64)
         for t in range(PACK):
@@ -140,9 +164,14 @@ def tile_list_tiert_none_kernel(
                 op=mybir.AluOpType.subtract,
             )
 
-        def second_tier(c, left):
+        def second_tier(c, left, w=W):
             codes, plane = tiers[("r", c)]
-            nc.vector.quantize_mx(out=codes[:].bitcast(FP8X4), scales=plane[:], in_=left[:])
+            for o in range(0, W, w):
+                nc.vector.quantize_mx(
+                    out=codes[:, o : o + w].bitcast(FP8X4),
+                    scales=plane[:, o : o + w],
+                    in_=left[:, PACK * o : PACK * (o + w)],
+                )
 
         planes = {}
 
@@ -217,26 +246,28 @@ def tile_list_tiert_none_kernel(
         pairs_of_tiles = [(m, m + 1) for m in range(0, N // P, 2)]
 
         left0 = lent([P, PACK * W], BF16, "left0", 20480)
-        low = round_x(0, HALF, nc.vector.tensor_copy, lent([P, PACK * HALF], BF16, "rounded0", 8192))
-        high = round_x(HALF, HALF, nc.scalar.copy, lent([P, PACK * HALF], BF16, "rounded128", 28672))
-        first_tier(HALF, HALF, high)
+        low = round_x(0, HALF, nc.vector.tensor_copy, lent([P, PACK * HALF], BF16, "rounded0", 8192 - 512))
+        mid = round_x(HALF, QUARTER, nc.vector.tensor_copy, lent([P, PACK * QUARTER], BF16, "rounded128", 8192 + 512))
+        high = round_x(HALF + QUARTER, QUARTER, nc.scalar.copy, own([P, PACK * QUARTER], BF16, "rounded192"))
+        first_tier(HALF + QUARTER, QUARTER, high)
         first_tier(0, HALF, low)
-        first01 = lent([P, 2 * W], U8, "first01", 28672)
+        first_tier(HALF, QUARTER, mid)
+        first01 = lent([P, 2 * W], U8, "first01", 8192 - 512)
         look_up_scales(0, 2, first01)
         shift_scales(0, 2, first01, nc.sync)
         load_x(W, W, 12288)
-        for s in (HALF, 0):
+        for s in (0, HALF):
             left_over(s, left0)
-        second_tier(0, left0)
+        second_tier(0, left0, HALF)
         load_x(2 * W, W, 32768)
         load_x(3 * W, W, 36864)
         for tier in ("q", "r"):
             for tiles in pairs_of_tiles:
                 passes(0, tiles, (tier,))
 
-        look_up_words(0, lent([P, W], U32, "pairs0", 21504), None)
-        first23 = lent([P, 2 * W], U8, "first23", 21504)
-        look_up_words(1, lent([P, W], U32, "pairs1", 22016), lambda: look_up_scales(2, 4, first23))
+        look_up_words(0, lent([P, W], U32, "pairs0", 0), None)
+        first23 = lent([P, 2 * W], U8, "first23", 0)
+        look_up_words(1, lent([P, W], U32, "pairs1", 512), lambda: look_up_scales(2, 4, first23))
         shift_scales(2, 4, first23, nc.sync)
         first_tier(W, W, round_x(W, W, nc.vector.tensor_copy, lent([P, PACK * W], BF16, "rounded256", 40960)))
         for a in range(2):

@@ -37,7 +37,7 @@ def tile_list_tiert_none_kernel(
         offsets = keep.tile([P, J // 16], U16, name="offsets")
         diag = lend.tile([P, 520], BF16, name="diag", align_bytes=64, offset=8192 + 448)
         tab_plane = keep.tile([P, T], U8, name="tab_plane", align_bytes=64)
-        wx_plane = keep.tile([P, N], U8, name="wx_plane", align_bytes=64)
+        wx_plane = keep.tile([P, N // 4], U8, name="wx_plane", align_bytes=64)
         tab = keep.tile([P, T], I32, name="tab", align_bytes=64)
         wx = keep.tile([P, N], I32, name="wx", align_bytes=64)
         wt = [keep.tile([P, 2 * N], U8, name="wt%d" % a, align_bytes=64) for a in range(2)]
@@ -71,8 +71,8 @@ def tile_list_tiert_none_kernel(
 
         def load_wx_scales(r, queue):
             queue.dma_start(
-                out=wx_plane[r:P:32, :].bitcast(I32),
-                in_=wx_scales[0].rearrange("(q r) n -> r q n", r=4)[r].bitcast(I32),
+                out=wx_plane[32 * r : 32 * r + 16, :].bitcast(I32),
+                in_=wx_scales[0, 4 * r : 4 * r + 4, :].rearrange("r (u n) -> u r n", u=4).bitcast(I32),
             )
 
         def load_wt_scales(r, queue):
@@ -82,30 +82,30 @@ def tile_list_tiert_none_kernel(
             )
 
         def load_tab(h):
-            cols = slice(h * T // 2, (h + 1) * T // 2)
+            cols = slice(h * T // 4, T if h else T // 4)
             nc.sync.dma_start(out=tab[:, cols], in_=tab_words[0, :, cols, :].rearrange("p t b -> p (t b)").bitcast(I32))
 
         def load_wt(a):
             nc.sync.dma_start(out=wt[a][:].bitcast(I32), in_=wt_words[a].bitcast(I32))
 
-        load_x(0, W, 0)
         nc.sync.dma_start(offsets[:], offs)
+        load_x(0, W, 0)
         load_tab_scales(0, nc.sync)
         load_tab_scales(1, nc.sync)
         load_tab_scales(2, nc.sync)
         load_tab_scales(3, nc.sync)
         nc.sync.dma_start(out=wx[:], in_=wx_words[0].rearrange("p n b -> p (n b)").bitcast(I32))
-        load_tab(0)
         load_wx_scales(0, nc.sync)
         load_wx_scales(1, nc.sync)
+        load_tab(0)
         load_wx_scales(2, nc.sync)
         load_wx_scales(3, nc.sync)
         load_tab(1)
-        load_wt(0)
         load_wt_scales(0, nc.sync)
         load_wt_scales(1, nc.sync)
         load_wt_scales(2, nc.sync)
         load_wt_scales(3, nc.sync)
+        load_wt(0)
         load_wt(1)
 
         eye = keep.tile([P, PACK, BANK], BF16, name="eye", align_bytes=64)
@@ -211,7 +211,7 @@ def tile_list_tiert_none_kernel(
                     if kind in ("q", "r"):
                         codes, plane = tiers[(kind, c)]
                         ops = dict(
-                            lhsT=wx[:, n0 : n0 + P].bitcast(FP8X4), lhsT_scale=wx_plane[:, n0 : n0 + P],
+                            lhsT=wx[:, n0 : n0 + P].bitcast(FP8X4), lhsT_scale=wx_plane[4 * (m // 2) : P, (m % 2) * P : (m % 2 + 1) * P],
                             rhs=codes[:].bitcast(FP8X4), rhs_scale=plane[:],
                         )
                     else:

@@ -81,15 +81,11 @@ def tile_list_tiert_none_kernel(
                 in_=wt_scales.rearrange("a (q r) n -> r q a n", r=4)[r].bitcast(I32),
             )
 
-        def load_tab(h):
-            cols = slice(h * T // 4, T if h else T // 4)
-            nc.sync.dma_start(out=tab[:, cols], in_=tab_words[0, :, cols, :].rearrange("p t b -> p (t b)").bitcast(I32))
-
         def load_wt(a):
             nc.sync.dma_start(out=wt[a][:].bitcast(I32), in_=wt_words[a].bitcast(I32))
 
-        nc.sync.dma_start(offsets[:], offs)
         load_x(0, W, 0)
+        nc.sync.dma_start(offsets[:], offs)
         load_tab_scales(0, nc.sync)
         load_tab_scales(1, nc.sync)
         load_tab_scales(2, nc.sync)
@@ -97,10 +93,9 @@ def tile_list_tiert_none_kernel(
         nc.sync.dma_start(out=wx[:], in_=wx_words[0].rearrange("p n b -> p (n b)").bitcast(I32))
         load_wx_scales(0, nc.sync)
         load_wx_scales(1, nc.sync)
-        load_tab(0)
         load_wx_scales(2, nc.sync)
         load_wx_scales(3, nc.sync)
-        load_tab(1)
+        nc.sync.dma_start(out=tab[:], in_=tab_words[0].rearrange("p t b -> p (t b)").bitcast(I32))
         load_wt_scales(0, nc.sync)
         load_wt_scales(1, nc.sync)
         load_wt_scales(2, nc.sync)
@@ -252,9 +247,9 @@ def tile_list_tiert_none_kernel(
         first_tier(HALF + QUARTER, QUARTER, high)
         first_tier(0, HALF, low)
         first_tier(HALF, QUARTER, mid)
-        first01 = lent([P, 2 * W], U8, "first01", 8192 - 512)
-        look_up_scales(0, 2, first01)
-        shift_scales(0, 2, first01, nc.sync)
+        first012 = lent([P, 3 * W], U8, "first012", 8192 - 512)
+        look_up_scales(0, 3, first012)
+        shift_scales(0, 3, first012, nc.sync)
         load_x(W, W, 12288)
         for s in (0, HALF):
             left_over(s, left0)
@@ -266,9 +261,9 @@ def tile_list_tiert_none_kernel(
                 passes(0, tiles, (tier,))
 
         look_up_words(0, lent([P, W], U32, "pairs0", 0), None)
-        first23 = lent([P, 2 * W], U8, "first23", 0)
-        look_up_words(1, lent([P, W], U32, "pairs1", 512), lambda: look_up_scales(2, 4, first23))
-        shift_scales(2, 4, first23, nc.sync)
+        first3 = lent([P, W], U8, "first3", 0)
+        look_up_words(1, lent([P, W], U32, "pairs1", 512), lambda: look_up_scales(3, 4, first3))
+        shift_scales(3, 4, first3, nc.sync)
         first_tier(W, W, round_x(W, W, nc.vector.tensor_copy, lent([P, PACK * W], BF16, "rounded256", 40960)))
         for a in range(2):
             for tiles in pairs_of_tiles:

@@ -111,15 +111,20 @@ def tile_list_tiert_none_kernel(
         nc.vector.quantize_mx(
             out=eye_codes[:].bitcast(FP8X4), scales=eye_plane[:], in_=eye[:].rearrange("p t c -> p (t c)")
         )
+        spans = [(0, W), (W, 2 * W), (3 * W, W)]
         tiers = {}
-        for c in range(J // W):
+        for g, (g0, gw) in enumerate(spans):
             for tier in ("q", "r"):
-                tiers[(tier, c)] = (
+                tiers[(tier, g)] = (
                     lend.tile([P, W], U32, name="codes_q0", align_bytes=64, offset=8192 + 1024)
-                    if (tier, c) == ("q", 0)
-                    else keep.tile([P, W], U32, name="codes_%s%d" % (tier, c), align_bytes=64),
-                    keep.tile([P, W], U8, name="plane_%s%d" % (tier, c), align_bytes=64),
+                    if (tier, g) == ("q", 0)
+                    else keep.tile([P, gw], U32, name="codes_%s%d" % (tier, g), align_bytes=64),
+                    keep.tile([P, gw], U8, name="plane_%s%d" % (tier, g), align_bytes=64),
                 )
+
+        def place(tier, j0):
+            g = max(i for i, span in enumerate(spans) if span[0] <= j0)
+            return tiers[(tier, g)] + (j0 - spans[g][0],)
 
         def woven(t):
             return t.rearrange("p (c i t) -> p c t i", i=NEAR, t=PACK)
@@ -133,14 +138,12 @@ def tile_list_tiert_none_kernel(
             return rounded
 
         def first_tier(j0, w, rounded):
-            codes, plane = tiers[("q", j0 // W)]
-            o = j0 % W
+            codes, plane, o = place("q", j0)
             nc.vector.quantize_mx(out=codes[:, o : o + w].bitcast(FP8X4), scales=plane[:, o : o + w], in_=rounded[:])
 
         def left_over(j0, left):
             tile, s = raw[j0]
-            c, o = divmod(j0, W)
-            codes, plane = tiers[("q", c)]
+            codes, plane, o = place("q", j0)
             deq = deq_pool.tile([P, PACK, HALF], F32, name="deq")
             for t in range(PACK):
                 nc.tensor.matmul_mx(
@@ -153,38 +156,38 @@ def tile_list_tiert_none_kernel(
                     stop=True,
                 )
             nc.vector.tensor_tensor(
-                out=woven(left[:, PACK * o : PACK * (o + HALF)]),
+                out=woven(left[:, PACK * s : PACK * (s + HALF)]),
                 in0=planar(tile[:, :, s : s + HALF]),
                 in1=planar(deq[:]),
                 op=mybir.AluOpType.subtract,
             )
 
         def second_tier(c, left, w=W):
-            codes, plane = tiers[("r", c)]
-            for o in range(0, W, w):
+            codes, plane, o = place("r", c * W)
+            for s in range(0, W, w):
                 nc.vector.quantize_mx(
-                    out=codes[:, o : o + w].bitcast(FP8X4),
-                    scales=plane[:, o : o + w],
-                    in_=left[:, PACK * o : PACK * (o + w)],
+                    out=codes[:, o + s : o + s + w].bitcast(FP8X4),
+                    scales=plane[:, o + s : o + s + w],
+                    in_=left[:, PACK * s : PACK * (s + w)],
                 )
 
         planes = {}
 
         def look_up_scales(c0, c1, first):
             nc.vector.tensor_copy(first[:], tab_plane[:].indirect(offsets[:, c0 * W // 16 : c1 * W // 16]))
-            for c in range(c0, c1):
-                planes[c] = (first[:, (c - c0) * W : (c - c0 + 1) * W], second[:, c * W : (c + 1) * W])
+            for g, (g0, gw) in enumerate(spans):
+                if c0 * W <= g0 < c1 * W:
+                    planes[g] = (first[:, g0 - c0 * W : g0 - c0 * W + gw], second[:, g0 : g0 + gw])
 
         def shift_scales(c0, c1, first, queue):
             queue.dma_start(out=second[0:112, c0 * W : c1 * W].bitcast(I32), in_=first[16:P, :].bitcast(I32))
 
         parted = {}
 
-        def look_up_words(c, pairs, between):
-            nc.vector.tensor_copy(pairs[:], tab[:].bitcast(U32).indirect(offsets[:, c * W // 16 : (c + 1) * W // 16]))
-            if between is not None:
-                between()
-            parted[c] = keep.tile([P, 2, 2 * W], U8, name="parted%d" % c, align_bytes=64)
+        def look_up_words(c, pairs):
+            g0, gw = spans[c]
+            nc.vector.tensor_copy(pairs[:], tab[:].bitcast(U32).indirect(offsets[:, g0 // 16 : (g0 + gw) // 16]))
+            parted[c] = keep.tile([P, 2, 2 * gw], U8, name="parted%d" % c, align_bytes=64)
             halves = pairs[:].bitcast(U16).rearrange("p (j d) -> p d j", d=2)
             if c == 0:
                 for a in range(2):
@@ -197,6 +200,7 @@ def tile_list_tiert_none_kernel(
 
         def passes(c, tiles, kinds):
             key = (c, tiles[0])
+            g0, gw = spans[c]
             if key not in banks:
                 banks[key] = acc_pool.tile([P, BANK], F32, name="acc")
                 done[key] = 0
@@ -216,17 +220,17 @@ def tile_list_tiert_none_kernel(
                             rhs=parted[c][:, kind, :].bitcast(FP4X4), rhs_scale=planes[c][kind],
                         )
                     nc.tensor.matmul_mx(
-                        out=banks[key][:, u * W : (u + 1) * W],
+                        out=banks[key][:, u * gw : (u + 1) * gw],
                         start=(done[key] == 0),
                         stop=(done[key] == 4 * len(tiles) - 1),
                         **ops,
                     )
                     done[key] = done[key] + 1
             if done[key] == 4 * len(tiles):
-                width = len(tiles) * W
+                width = len(tiles) * gw
                 result = stage.tile([P, width], F32, name="result")
                 nc.scalar.copy(out=result[:], in_=banks[key][:, 0:width])
-                rows = out[tiles[0] * P : (tiles[-1] + 1) * P, c * W : (c + 1) * W]
+                rows = out[tiles[0] * P : (tiles[-1] + 1) * P, g0 : g0 + gw]
                 nc.sync.dma_start(
                     out=rows.rearrange("(u p) j -> p u j", p=P),
                     in_=result[:].rearrange("p (u j) -> p u j", u=len(tiles)),
@@ -260,39 +264,40 @@ def tile_list_tiert_none_kernel(
             for tiles in pairs_of_tiles:
                 passes(0, tiles, (tier,))
 
-        look_up_words(0, lent([P, W], U32, "pairs0", 0), None)
-        first3 = lent([P, W], U8, "first3", 0)
-        look_up_words(1, lent([P, W], U32, "pairs1", 512), lambda: look_up_scales(3, 4, first3))
-        shift_scales(3, 4, first3, nc.sync)
+        look_up_words(0, lent([P, W], U32, "pairs0", 0))
+        look_up_words(1, lent([P, 2 * W], U32, "pairs1", 512))
         first_tier(W, W, round_x(W, W, nc.vector.tensor_copy, lent([P, PACK * W], BF16, "rounded256", 40960)))
+        first3 = lent([P, W], U8, "first3", 40960)
+        look_up_scales(3, 4, first3)
+        shift_scales(3, 4, first3, nc.sync)
         for a in range(2):
             for tiles in pairs_of_tiles:
                 passes(0, tiles, (a,))
-        for tiles in pairs_of_tiles[:2]:
-            passes(1, tiles, (1, 0))
+        for m in range(2):
+            passes(1, (m,), (1, 0))
         left1 = lent([P, PACK * W], BF16, "left1", 24576)
         left_over(W, left1)
         left_over(W + HALF, left1)
-        second_tier(1, left1)
-        look_up_words(2, lent([P, W], U32, "pairs2", 40960), None)
         first_tier(2 * W, W, round_x(2 * W, W, nc.scalar.copy, lent([P, PACK * W], BF16, "rounded512", 16384)))
-        for tiles in pairs_of_tiles[2:]:
-            passes(1, tiles, (0, 1))
+        second_tier(1, left1)
+        look_up_words(2, lent([P, W], U32, "pairs3", 24576))
+        for m in range(2, 4):
+            passes(1, (m,), (0, 1))
         left2 = own([P, PACK * W], BF16, "left2")
         left_over(2 * W, left2)
         left_over(2 * W + HALF, left2)
-        second_tier(2, left2)
-        look_up_words(3, lent([P, W], U32, "pairs3", 24576), None)
         first_tier(3 * W, W, round_x(3 * W, W, nc.scalar.copy, lent([P, PACK * W], BF16, "rounded768", 17408)))
-        for tiles in pairs_of_tiles:
-            passes(1, tiles, ("q", "r"))
-        for tiles in pairs_of_tiles[:2]:
-            passes(2, tiles, (0, 1, "q", "r"))
+        second_tier(2, left2)
+        for m in range(4, 6):
+            passes(1, (m,), (0, 1))
+        for tier in ("q", "r"):
+            for m in range(6):
+                passes(1, (m,), (tier,))
         left3 = own([P, PACK * W], BF16, "left3")
         left_over(3 * W, left3)
         left_over(3 * W + HALF, left3)
         second_tier(3, left3)
-        for tiles in pairs_of_tiles[2:]:
-            passes(2, tiles, (0, 1, "q", "r"))
+        for m in range(6, 8):
+            passes(1, (m,), (0, 1, "q", "r"))
         for tiles in pairs_of_tiles[:3] + [(6,), (7,)]:
-            passes(3, tiles, (0, 1, "q", "r"))
+            passes(2, tiles, (0, 1, "q", "r"))

@@ -189,8 +189,8 @@ def tile_list_tiert_none_kernel(
             nc.vector.tensor_copy(pairs[:], tab[:].bitcast(U32).indirect(offsets[:, g0 // 16 : (g0 + gw) // 16]))
             parted[c] = keep.tile([P, 2, 2 * gw], U8, name="parted%d" % c, align_bytes=64)
             halves = pairs[:].bitcast(U16).rearrange("p (j d) -> p d j", d=2)
-            if c == 0:
-                for a in range(2):
+            if c < 2:
+                for a in ((0, 1), (1, 0))[c]:
                     nc.vector.tensor_copy(out=parted[c][:, a, :].bitcast(U16), in_=halves[:, a, :])
             else:
                 nc.vector.tensor_copy(out=parted[c][:].bitcast(U16), in_=halves)
@@ -273,21 +273,20 @@ def tile_list_tiert_none_kernel(
         for a in range(2):
             for tiles in pairs_of_tiles:
                 passes(0, tiles, (a,))
-        for m in range(2):
+        for m in range(3):
             passes(1, (m,), (1, 0))
         left1 = lent([P, PACK * W], BF16, "left1", 24576)
         left_over(W, left1)
         left_over(W + HALF, left1)
         first_tier(2 * W, W, round_x(2 * W, W, nc.scalar.copy, lent([P, PACK * W], BF16, "rounded512", 16384)))
         second_tier(1, left1)
-        look_up_words(2, lent([P, W], U32, "pairs3", 24576))
-        for m in range(2, 4):
-            passes(1, (m,), (0, 1))
-        left2 = own([P, PACK * W], BF16, "left2")
+        passes(1, (3,), (0, 1))
+        left2 = lent([P, PACK * W], BF16, "left2", 45056)
         left_over(2 * W, left2)
         left_over(2 * W + HALF, left2)
-        first_tier(3 * W, W, round_x(3 * W, W, nc.scalar.copy, lent([P, PACK * W], BF16, "rounded768", 17408)))
         second_tier(2, left2)
+        first_tier(3 * W, W, round_x(3 * W, W, nc.scalar.copy, lent([P, PACK * W], BF16, "rounded768", 17408)))
+        look_up_words(2, lent([P, W], U32, "pairs3", 45056))
         for m in range(4, 6):
             passes(1, (m,), (0, 1))
         for tier in ("q", "r"):

@@ -44,8 +44,8 @@ def tile_list_tiert_none_kernel(
         second = keep.tile([P, J], U8, name="second", align_bytes=64)
 
         wt_plane = keep.tile([P, 2 * N], U8, name="wt_plane", align_bytes=64)
-        nc.vector.memset(tab_plane[:].bitcast(I32), 0)
         nc.vector.memset(wx_plane[:].bitcast(I32), 0)
+        nc.vector.memset(tab_plane[:].bitcast(I32), 0)
         nc.vector.memset(wt_plane[:].bitcast(I32), 0)
         nc.vector.memset(second[:].bitcast(I32), 0)
 
@@ -85,16 +85,17 @@ def tile_list_tiert_none_kernel(
             nc.sync.dma_start(out=wt[a][:].bitcast(I32), in_=wt_words[a].bitcast(I32))
 
         load_x(0, W, 0)
-        nc.sync.dma_start(offsets[:], offs)
-        load_tab_scales(0, nc.sync)
-        load_tab_scales(1, nc.sync)
-        load_tab_scales(2, nc.sync)
-        load_tab_scales(3, nc.sync)
-        nc.sync.dma_start(out=wx[:], in_=wx_words[0].rearrange("p n b -> p (n b)").bitcast(I32))
         load_wx_scales(0, nc.sync)
         load_wx_scales(1, nc.sync)
         load_wx_scales(2, nc.sync)
         load_wx_scales(3, nc.sync)
+        nc.sync.dma_start(out=wx[:], in_=wx_words[0].rearrange("p n b -> p (n b)").bitcast(I32))
+        nc.sync.dma_start(offsets[:], offs)
+        load_x(W, W, 12288)
+        load_tab_scales(0, nc.sync)
+        load_tab_scales(1, nc.sync)
+        load_tab_scales(2, nc.sync)
+        load_tab_scales(3, nc.sync)
         nc.sync.dma_start(out=tab[:], in_=tab_words[0].rearrange("p t b -> p (t b)").bitcast(I32))
         load_wt_scales(0, nc.sync)
         load_wt_scales(1, nc.sync)
@@ -111,13 +112,13 @@ def tile_list_tiert_none_kernel(
         nc.vector.quantize_mx(
             out=eye_codes[:].bitcast(FP8X4), scales=eye_plane[:], in_=eye[:].rearrange("p t c -> p (t c)")
         )
-        spans = [(0, W), (W, 2 * W), (3 * W, W)]
+        spans = [(0, W), (W, W), (2 * W, W), (3 * W, W)]
         tiers = {}
         for g, (g0, gw) in enumerate(spans):
             for tier in ("q", "r"):
                 tiers[(tier, g)] = (
-                    lend.tile([P, W], U32, name="codes_q0", align_bytes=64, offset=8192 + 1024)
-                    if (tier, g) == ("q", 0)
+                    lend.tile([P, W], U32, name="codes_q%d" % g, align_bytes=64, offset=(8192 + 1024, 21504)[g])
+                    if tier == "q" and g < 2
                     else keep.tile([P, gw], U32, name="codes_%s%d" % (tier, g), align_bytes=64),
                     keep.tile([P, gw], U8, name="plane_%s%d" % (tier, g), align_bytes=64),
                 )
@@ -141,8 +142,7 @@ def tile_list_tiert_none_kernel(
             codes, plane, o = place("q", j0)
             nc.vector.quantize_mx(out=codes[:, o : o + w].bitcast(FP8X4), scales=plane[:, o : o + w], in_=rounded[:])
 
-        def left_over(j0, left):
-            tile, s = raw[j0]
+        def give_back(j0):
             codes, plane, o = place("q", j0)
             deq = deq_pool.tile([P, PACK, HALF], F32, name="deq")
             for t in range(PACK):
@@ -155,6 +155,11 @@ def tile_list_tiert_none_kernel(
                     start=True,
                     stop=True,
                 )
+            return deq
+
+        def left_over(j0, left, deq=None):
+            tile, s = raw[j0]
+            deq = give_back(j0) if deq is None else deq
             nc.vector.tensor_tensor(
                 out=woven(left[:, PACK * s : PACK * (s + HALF)]),
                 in0=planar(tile[:, :, s : s + HALF]),
@@ -184,13 +189,15 @@ def tile_list_tiert_none_kernel(
 
         parted = {}
 
-        def look_up_words(c, pairs):
+        def look_up_words(c, pairs, between=None):
             g0, gw = spans[c]
             nc.vector.tensor_copy(pairs[:], tab[:].bitcast(U32).indirect(offsets[:, g0 // 16 : (g0 + gw) // 16]))
+            if between is not None:
+                between()
             parted[c] = keep.tile([P, 2, 2 * gw], U8, name="parted%d" % c, align_bytes=64)
             halves = pairs[:].bitcast(U16).rearrange("p (j d) -> p d j", d=2)
-            if c < 2:
-                for a in ((0, 1), (1, 0))[c]:
+            if c == 0:
+                for a in range(2):
                     nc.vector.tensor_copy(out=parted[c][:, a, :].bitcast(U16), in_=halves[:, a, :])
             else:
                 nc.vector.tensor_copy(out=parted[c][:].bitcast(U16), in_=halves)
@@ -251,52 +258,55 @@ def tile_list_tiert_none_kernel(
         first_tier(HALF + QUARTER, QUARTER, high)
         first_tier(0, HALF, low)
         first_tier(HALF, QUARTER, mid)
-        first012 = lent([P, 3 * W], U8, "first012", 8192 - 512)
-        look_up_scales(0, 3, first012)
-        shift_scales(0, 3, first012, nc.sync)
-        load_x(W, W, 12288)
+        rounded1 = round_x(W, W, nc.scalar.copy, lent([P, PACK * W], BF16, "rounded256", 51200))
         for s in (0, HALF):
             left_over(s, left0)
         second_tier(0, left0, HALF)
+        first01 = lent([P, 2 * W], U8, "first01", 20480)
+        look_up_scales(0, 2, first01)
+        shift_scales(0, 2, first01, nc.sync)
+        first_tier(W, W, rounded1)
         load_x(2 * W, W, 32768)
         load_x(3 * W, W, 36864)
         for tier in ("q", "r"):
             for tiles in pairs_of_tiles:
                 passes(0, tiles, (tier,))
 
-        look_up_words(0, lent([P, W], U32, "pairs0", 0))
-        look_up_words(1, lent([P, 2 * W], U32, "pairs1", 512))
-        first_tier(W, W, round_x(W, W, nc.vector.tensor_copy, lent([P, PACK * W], BF16, "rounded256", 40960)))
-        first3 = lent([P, W], U8, "first3", 40960)
-        look_up_scales(3, 4, first3)
-        shift_scales(3, 4, first3, nc.sync)
+        given = [give_back(W), give_back(W + HALF)]
+        for tiles in pairs_of_tiles[:2]:
+            passes(1, tiles, ("q",))
+        look_up_words(0, lent([P, W], U32, "pairs0", 51200))
+        left1 = lent([P, PACK * W], BF16, "left1", 49664)
+        look_up_words(1, lent([P, W], U32, "pairs1", 51712), lambda: left_over(W, left1, given[0]))
+        left_over(W + HALF, left1, given[1])
+        second_tier(1, left1, HALF)
+        first23 = lent([P, 2 * W], U8, "first23", 49664)
+        look_up_scales(2, 4, first23)
+        shift_scales(2, 4, first23, nc.sync)
+        first_tier(2 * W, W, round_x(2 * W, W, nc.scalar.copy, lent([P, PACK * W], BF16, "rounded512", 16384)))
+        look_up_words(2, lent([P, W], U32, "pairs2", 16384))
         for a in range(2):
             for tiles in pairs_of_tiles:
                 passes(0, tiles, (a,))
-        for m in range(3):
-            passes(1, (m,), (1, 0))
-        left1 = lent([P, PACK * W], BF16, "left1", 24576)
-        left_over(W, left1)
-        left_over(W + HALF, left1)
-        first_tier(2 * W, W, round_x(2 * W, W, nc.scalar.copy, lent([P, PACK * W], BF16, "rounded512", 16384)))
-        second_tier(1, left1)
-        passes(1, (3,), (0, 1))
+        for tiles in pairs_of_tiles[:2]:
+            passes(1, tiles, (1, 0))
+        for tiles in pairs_of_tiles[:2]:
+            passes(1, tiles, ("r",))
+        passes(1, pairs_of_tiles[2], (0, 1, "q", "r"))
         left2 = lent([P, PACK * W], BF16, "left2", 45056)
         left_over(2 * W, left2)
         left_over(2 * W + HALF, left2)
-        second_tier(2, left2)
+        second_tier(2, left2, HALF)
         first_tier(3 * W, W, round_x(3 * W, W, nc.scalar.copy, lent([P, PACK * W], BF16, "rounded768", 17408)))
-        look_up_words(2, lent([P, W], U32, "pairs3", 45056))
-        for m in range(4, 6):
-            passes(1, (m,), (0, 1))
-        for tier in ("q", "r"):
-            for m in range(6):
-                passes(1, (m,), (tier,))
+        look_up_words(3, lent([P, W], U32, "pairs3", 45056))
+        passes(1, pairs_of_tiles[3], (0, 1, "q", "r"))
+        for tiles in pairs_of_tiles[:2]:
+            passes(2, tiles, (0, 1, "q", "r"))
         left3 = own([P, PACK * W], BF16, "left3")
         left_over(3 * W, left3)
         left_over(3 * W + HALF, left3)
         second_tier(3, left3)
-        for m in range(6, 8):
-            passes(1, (m,), (0, 1, "q", "r"))
-        for tiles in pairs_of_tiles[:3] + [(6,), (7,)]:
+        for tiles in pairs_of_tiles[2:]:
             passes(2, tiles, (0, 1, "q", "r"))
+        for tiles in pairs_of_tiles[:3] + [(6,), (7,)]:
+            passes(3, tiles, (0, 1, "q", "r"))

@@ -31,8 +31,10 @@ def tile_list_tiert_none_kernel(
         keep = ctx.enter_context(tc.tile_pool(name="keep", bufs=1))
         lend = ctx.enter_context(tc.tile_pool(name="lend", bufs=1))
         stage = ctx.enter_context(tc.tile_pool(name="stage", bufs=8))
-        acc_pool = ctx.enter_context(tc.psum_pool(name="acc", bufs=6))
-        deq_pool = ctx.enter_context(tc.psum_pool(name="deq", bufs=2))
+        psum = ctx.enter_context(tc.psum_pool(name="psum", bufs=1))
+
+        def bank(shape, name, b):
+            return psum.tile(shape, F32, name=name, offset=2048 * b)
 
         offsets = keep.tile([P, J // 16], U16, name="offsets")
         diag = lend.tile([P, 520], BF16, name="diag", align_bytes=64, offset=8192 + 448)
@@ -104,14 +106,28 @@ def tile_list_tiert_none_kernel(
         load_wt(0)
         load_wt(1)
 
-        eye = keep.tile([P, PACK, BANK], BF16, name="eye", align_bytes=64)
-        for t in range(PACK):
-            nc.vector.tensor_copy(out=eye[:, t, :], in_=diag[:, 3 - t : 3 - t + BANK])
+        eye = keep.tile([P, PACK - 1, BANK], BF16, name="eye", align_bytes=64)
         eye_codes = keep.tile([P, BANK], U32, name="eye_codes", align_bytes=64)
         eye_plane = keep.tile([P, BANK], U8, name="eye_plane", align_bytes=64)
-        nc.vector.quantize_mx(
-            out=eye_codes[:].bitcast(FP8X4), scales=eye_plane[:], in_=eye[:].rearrange("p t c -> p (t c)")
-        )
+
+        def quantise_eye(t0, t1, values):
+            nc.vector.quantize_mx(
+                out=eye_codes[:, t0 * P : t1 * P].bitcast(FP8X4), scales=eye_plane[:, t0 * P : t1 * P], in_=values
+            )
+
+        quantise_eye(3, 4, diag[:, 0:BANK])
+        for t in range(PACK - 1):
+            nc.vector.tensor_copy(out=eye[:, t, :], in_=diag[:, 3 - t : 3 - t + BANK])
+        quantise_eye(0, 2, eye[:, 0:2, :].rearrange("p t c -> p (t c)"))
+        quantise_eye(2, 3, eye[:, 2, :])
+        idle = bank([P, PACK, HALF], "idle", 7)
+        for i in range(10):
+            nc.tensor.matmul_mx(
+                out=idle[:, i % PACK, :],
+                lhsT=eye_codes[:, 3 * P : 4 * P].bitcast(FP8X4), lhsT_scale=eye_plane[:, 3 * P : 4 * P],
+                rhs=eye_codes[:, 3 * P : 4 * P].bitcast(FP8X4), rhs_scale=eye_plane[:, 3 * P : 4 * P],
+                start=True, stop=True,
+            )
         spans = [(0, W), (W, W), (2 * W, W), (3 * W, W)]
         tiers = {}
         for g, (g0, gw) in enumerate(spans):
@@ -144,7 +160,7 @@ def tile_list_tiert_none_kernel(
 
         def give_back(j0):
             codes, plane, o = place("q", j0)
-            deq = deq_pool.tile([P, PACK, HALF], F32, name="deq")
+            deq = bank([P, PACK, HALF], "deq%d" % j0, (6 if j0 < 2 * W else 0) + j0 // HALF % 2)
             for t in range(PACK):
                 nc.tensor.matmul_mx(
                     out=deq[:, t, :],
@@ -179,7 +195,7 @@ def tile_list_tiert_none_kernel(
         planes = {}
 
         def look_up_scales(c0, c1, first):
-            nc.vector.tensor_copy(first[:], tab_plane[:].indirect(offsets[:, c0 * W // 16 : c1 * W // 16]))
+            nc.vector.tensor_copy(first, tab_plane[:].indirect(offsets[:, c0 * W // 16 : c1 * W // 16]))
             for g, (g0, gw) in enumerate(spans):
                 if c0 * W <= g0 < c1 * W:
                     planes[g] = (first[:, g0 - c0 * W : g0 - c0 * W + gw], second[:, g0 : g0 + gw])
@@ -203,13 +219,18 @@ def tile_list_tiert_none_kernel(
                 nc.vector.tensor_copy(out=parted[c][:].bitcast(U16), in_=halves)
 
         banks = {}
+        homes = {}
+        for c, row in enumerate(((0, 1, 2, 3), (4, 5, 6, 7), (2, 3, 4, 5), (6, 7, 2, 3))):
+            for i, b in enumerate(row):
+                homes[(c, 2 * i)] = b
+        homes[(3, 7)] = 4
         done = {}
 
         def passes(c, tiles, kinds):
             key = (c, tiles[0])
             g0, gw = spans[c]
             if key not in banks:
-                banks[key] = acc_pool.tile([P, BANK], F32, name="acc")
+                banks[key] = bank([P, BANK], "acc%d_%d" % key, homes[key])
                 done[key] = 0
             for kind in kinds:
                 for u, m in enumerate(tiles):
@@ -263,17 +284,22 @@ def tile_list_tiert_none_kernel(
             left_over(s, left0)
         second_tier(0, left0, HALF)
         first01 = lent([P, 2 * W], U8, "first01", 20480)
-        look_up_scales(0, 2, first01)
-        shift_scales(0, 2, first01, nc.sync)
+        look_up_scales(0, 1, first01[:, 0:W])
         first_tier(W, W, rounded1)
+        look_up_scales(1, 2, first01[:, W : 2 * W])
+        shift_scales(0, 2, first01, nc.sync)
         load_x(2 * W, W, 32768)
         load_x(3 * W, W, 36864)
         for tier in ("q", "r"):
             for tiles in pairs_of_tiles:
                 passes(0, tiles, (tier,))
 
-        given = [give_back(W), give_back(W + HALF)]
-        for tiles in pairs_of_tiles[:2]:
+        given = []
+        for s in (0, HALF):
+            deq = give_back(W + s)
+            given.append(own([P, PACK, HALF], F32, "given%d" % s))
+            nc.scalar.copy(out=given[-1][:], in_=deq[:])
+        for tiles in pairs_of_tiles:
             passes(1, tiles, ("q",))
         look_up_words(0, lent([P, W], U32, "pairs0", 51200))
         left1 = lent([P, PACK * W], BF16, "left1", 49664)
@@ -281,32 +307,33 @@ def tile_list_tiert_none_kernel(
         left_over(W + HALF, left1, given[1])
         second_tier(1, left1, HALF)
         first23 = lent([P, 2 * W], U8, "first23", 49664)
-        look_up_scales(2, 4, first23)
+        look_up_scales(2, 4, first23[:])
         shift_scales(2, 4, first23, nc.sync)
         first_tier(2 * W, W, round_x(2 * W, W, nc.scalar.copy, lent([P, PACK * W], BF16, "rounded512", 16384)))
         look_up_words(2, lent([P, W], U32, "pairs2", 16384))
         for a in range(2):
             for tiles in pairs_of_tiles:
                 passes(0, tiles, (a,))
-        for tiles in pairs_of_tiles[:2]:
+        for tiles in pairs_of_tiles:
             passes(1, tiles, (1, 0))
-        for tiles in pairs_of_tiles[:2]:
+        for tiles in pairs_of_tiles:
             passes(1, tiles, ("r",))
-        passes(1, pairs_of_tiles[2], (0, 1, "q", "r"))
         left2 = lent([P, PACK * W], BF16, "left2", 45056)
         left_over(2 * W, left2)
         left_over(2 * W + HALF, left2)
         second_tier(2, left2, HALF)
         first_tier(3 * W, W, round_x(3 * W, W, nc.scalar.copy, lent([P, PACK * W], BF16, "rounded768", 17408)))
         look_up_words(3, lent([P, W], U32, "pairs3", 45056))
-        passes(1, pairs_of_tiles[3], (0, 1, "q", "r"))
-        for tiles in pairs_of_tiles[:2]:
-            passes(2, tiles, (0, 1, "q", "r"))
+        for kind in ("q", 0, 1):
+            for tiles in pairs_of_tiles[:2]:
+                passes(2, tiles, (kind,))
+        passes(2, pairs_of_tiles[2], ("q", 0, 1))
         left3 = own([P, PACK * W], BF16, "left3")
         left_over(3 * W, left3)
         left_over(3 * W + HALF, left3)
         second_tier(3, left3)
-        for tiles in pairs_of_tiles[2:]:
-            passes(2, tiles, (0, 1, "q", "r"))
+        for tiles in pairs_of_tiles[:3]:
+            passes(2, tiles, ("r",))
+        passes(2, pairs_of_tiles[3], (0, 1, "q", "r"))
         for tiles in pairs_of_tiles[:3] + [(6,), (7,)]:
             passes(3, tiles, (0, 1, "q", "r"))

@@ -120,14 +120,6 @@ def tile_list_tiert_none_kernel(
             nc.vector.tensor_copy(out=eye[:, t, :], in_=diag[:, 3 - t : 3 - t + BANK])
         quantise_eye(0, 2, eye[:, 0:2, :].rearrange("p t c -> p (t c)"))
         quantise_eye(2, 3, eye[:, 2, :])
-        idle = bank([P, PACK, HALF], "idle", 7)
-        for i in range(10):
-            nc.tensor.matmul_mx(
-                out=idle[:, i % PACK, :],
-                lhsT=eye_codes[:, 3 * P : 4 * P].bitcast(FP8X4), lhsT_scale=eye_plane[:, 3 * P : 4 * P],
-                rhs=eye_codes[:, 3 * P : 4 * P].bitcast(FP8X4), rhs_scale=eye_plane[:, 3 * P : 4 * P],
-                start=True, stop=True,
-            )
         spans = [(0, W), (W, W), (2 * W, W), (3 * W, W)]
         tiers = {}
         for g, (g0, gw) in enumerate(spans):

@@ -20,7 +20,7 @@ BANK = 512
 W = 256
 HALF = 128
 QUARTER = 64
-NEAR = 2
+NEAR = 4
 
 
 def tile_list_tiert_none_kernel(

@@ -21,6 +21,7 @@ W = 256
 HALF = 128
 QUARTER = 64
 NEAR = 4
+FIXED_CODES, FIXED_SCALES, MOVING_CODES, MOVING_SCALES = 0, 64, 128, 192
 
 
 def tile_list_tiert_none_kernel(
@@ -30,22 +31,31 @@ def tile_list_tiert_none_kernel(
     with ExitStack() as ctx:
         keep = ctx.enter_context(tc.tile_pool(name="keep", bufs=1))
         lend = ctx.enter_context(tc.tile_pool(name="lend", bufs=1))
+        spread = ctx.enter_context(tc.tile_pool(name="spread", bufs=1))
         stage = ctx.enter_context(tc.tile_pool(name="stage", bufs=8))
         psum = ctx.enter_context(tc.psum_pool(name="psum", bufs=1))
 
         def bank(shape, name, b):
             return psum.tile(shape, F32, name=name, offset=2048 * b)
 
+        taken = [4 * N]
+
+        def operand(columns, dtype, name, phase):
+            size = columns * (1 if dtype == U8 else 4)
+            start = taken[-1] + phase
+            taken.append((start + size + 255) // 256 * 256)
+            return spread.tile([P, columns], dtype, name=name, align_bytes=64, offset=start)
+
         offsets = keep.tile([P, J // 16], U16, name="offsets")
         diag = lend.tile([P, 520], BF16, name="diag", align_bytes=64, offset=8192 + 448)
         tab_plane = keep.tile([P, T], U8, name="tab_plane", align_bytes=64)
-        wx_plane = keep.tile([P, N // 4], U8, name="wx_plane", align_bytes=64)
+        wx_plane = operand(N // 4, U8, "wx_plane", FIXED_SCALES)
         tab = keep.tile([P, T], I32, name="tab", align_bytes=64)
-        wx = keep.tile([P, N], I32, name="wx", align_bytes=64)
-        wt = [keep.tile([P, 2 * N], U8, name="wt%d" % a, align_bytes=64) for a in range(2)]
-        second = keep.tile([P, J], U8, name="second", align_bytes=64)
+        wx = spread.tile([P, N], I32, name="wx", align_bytes=256, offset=0)
+        wt = [operand(2 * N, U8, "wt%d" % a, FIXED_CODES) for a in range(2)]
+        second = operand(J, U8, "second", MOVING_SCALES)
 
-        wt_plane = keep.tile([P, 2 * N], U8, name="wt_plane", align_bytes=64)
+        wt_plane = operand(2 * N, U8, "wt_plane", FIXED_SCALES)
         nc.vector.memset(wx_plane[:].bitcast(I32), 0)
         nc.vector.memset(tab_plane[:].bitcast(I32), 0)
         nc.vector.memset(wt_plane[:].bitcast(I32), 0)
@@ -60,7 +70,7 @@ def tile_list_tiert_none_kernel(
         raw = {}
 
         def load_x(j0, w, offset):
-            tile = lend.tile([P, PACK, w], F32, name="raw%d" % j0, align_bytes=64, offset=offset)
+            tile = lend.tile([P, PACK, w], F32, name="raw%d" % j0, align_bytes=256, offset=offset)
             nc.sync.dma_start(out=tile[:], in_=x[:, j0 : j0 + w].rearrange("(p t) j -> p t j", t=PACK))
             for s in range(0, w, QUARTER):
                 raw[j0 + s] = (tile, s)
@@ -107,8 +117,8 @@ def tile_list_tiert_none_kernel(
         load_wt(1)
 
         eye = keep.tile([P, PACK - 1, BANK], BF16, name="eye", align_bytes=64)
-        eye_codes = keep.tile([P, BANK], U32, name="eye_codes", align_bytes=64)
-        eye_plane = keep.tile([P, BANK], U8, name="eye_plane", align_bytes=64)
+        eye_codes = operand(BANK, U32, "eye_codes", FIXED_CODES)
+        eye_plane = operand(BANK, U8, "eye_plane", FIXED_SCALES)
 
         def quantise_eye(t0, t1, values):
             nc.vector.quantize_mx(
@@ -125,10 +135,10 @@ def tile_list_tiert_none_kernel(
         for g, (g0, gw) in enumerate(spans):
             for tier in ("q", "r"):
                 tiers[(tier, g)] = (
-                    lend.tile([P, W], U32, name="codes_q%d" % g, align_bytes=64, offset=(8192 + 1024, 21504)[g])
+                    lend.tile([P, W], U32, name="codes_q%d" % g, align_bytes=64, offset=(8192 + 1024, 21504)[g] + MOVING_CODES)
                     if tier == "q" and g < 2
-                    else keep.tile([P, gw], U32, name="codes_%s%d" % (tier, g), align_bytes=64),
-                    keep.tile([P, gw], U8, name="plane_%s%d" % (tier, g), align_bytes=64),
+                    else operand(gw, U32, "codes_%s%d" % (tier, g), MOVING_CODES),
+                    operand(gw, U8, "plane_%s%d" % (tier, g), MOVING_SCALES),
                 )
 
         def place(tier, j0):
@@ -202,13 +212,13 @@ def tile_list_tiert_none_kernel(
             nc.vector.tensor_copy(pairs[:], tab[:].bitcast(U32).indirect(offsets[:, g0 // 16 : (g0 + gw) // 16]))
             if between is not None:
                 between()
-            parted[c] = keep.tile([P, 2, 2 * gw], U8, name="parted%d" % c, align_bytes=64)
+            parted[c] = operand(4 * gw, U8, "parted%d" % c, MOVING_CODES)[:].rearrange("p (a w) -> p a w", a=2)
             halves = pairs[:].bitcast(U16).rearrange("p (j d) -> p d j", d=2)
             if c == 0:
                 for a in range(2):
                     nc.vector.tensor_copy(out=parted[c][:, a, :].bitcast(U16), in_=halves[:, a, :])
             else:
-                nc.vector.tensor_copy(out=parted[c][:].bitcast(U16), in_=halves)
+                nc.vector.tensor_copy(out=parted[c].bitcast(U16), in_=halves)
 
         banks = {}
         homes = {}
@@ -275,7 +285,7 @@ def tile_list_tiert_none_kernel(
         for s in (0, HALF):
             left_over(s, left0)
         second_tier(0, left0, HALF)
-        first01 = lent([P, 2 * W], U8, "first01", 20480)
+        first01 = lent([P, 2 * W], U8, "first01", 20480 + MOVING_SCALES)
         look_up_scales(0, 1, first01[:, 0:W])
         first_tier(W, W, rounded1)
         look_up_scales(1, 2, first01[:, W : 2 * W])
@@ -298,7 +308,7 @@ def tile_list_tiert_none_kernel(
         look_up_words(1, lent([P, W], U32, "pairs1", 51712), lambda: left_over(W, left1, given[0]))
         left_over(W + HALF, left1, given[1])
         second_tier(1, left1, HALF)
-        first23 = lent([P, 2 * W], U8, "first23", 49664)
+        first23 = lent([P, 2 * W], U8, "first23", 49664 + MOVING_SCALES)
         look_up_scales(2, 4, first23[:])
         shift_scales(2, 4, first23, nc.sync)
         first_tier(2 * W, W, round_x(2 * W, W, nc.scalar.copy, lent([P, PACK * W], BF16, "rounded512", 16384)))

@@ -225,12 +225,20 @@ def tile_list_tiert_none_kernel(
         for c, row in enumerate(((0, 1, 2, 3), (4, 5, 6, 7), (2, 3, 4, 5), (6, 7, 2, 3))):
             for i, b in enumerate(row):
                 homes[(c, 2 * i)] = b
-        homes[(3, 7)] = 4
+        for i, b in enumerate((0, 1, 2, 3, 4)):
+            homes[(3, 4 + i)] = b
+        joint = [keep.tile([P, 2 * BANK], F32, name="joint%d" % i) for i in range(2)]
         done = {}
 
-        def passes(c, tiles, kinds):
-            key = (c, tiles[0])
-            g0, gw = spans[c]
+        def store(result, m, count, g0, gw):
+            nc.sync.dma_start(
+                out=out[m * P : (m + count) * P, g0 : g0 + gw].rearrange("(u p) j -> p u j", p=P),
+                in_=result[:].rearrange("p (u j) -> p u j", u=count),
+            )
+
+        def passes(c, tiles, kinds, s0=0, gw=W):
+            key = (c, tiles[0] + s0 // HALF)
+            g0 = c * W + s0
             if key not in banks:
                 banks[key] = bank([P, BANK], "acc%d_%d" % key, homes[key])
                 done[key] = 0
@@ -241,13 +249,14 @@ def tile_list_tiert_none_kernel(
                         codes, plane = tiers[(kind, c)]
                         ops = dict(
                             lhsT=wx[:, n0 : n0 + P].bitcast(FP8X4), lhsT_scale=wx_plane[4 * (m // 2) : P, (m % 2) * P : (m % 2 + 1) * P],
-                            rhs=codes[:].bitcast(FP8X4), rhs_scale=plane[:],
+                            rhs=codes[:, s0 : s0 + gw].bitcast(FP8X4), rhs_scale=plane[:, s0 : s0 + gw],
                         )
                     else:
                         ops = dict(
                             lhsT=wt[kind][:, 2 * n0 : 2 * (n0 + P)].bitcast(FP4X4),
                             lhsT_scale=wt_plane[:, kind * N + n0 : kind * N + n0 + P],
-                            rhs=parted[c][:, kind, :].bitcast(FP4X4), rhs_scale=planes[c][kind],
+                            rhs=parted[c][:, kind, 2 * s0 : 2 * (s0 + gw)].bitcast(FP4X4),
+                            rhs_scale=planes[c][kind][:, s0 : s0 + gw],
                         )
                     nc.tensor.matmul_mx(
                         out=banks[key][:, u * gw : (u + 1) * gw],
@@ -258,13 +267,16 @@ def tile_list_tiert_none_kernel(
                     done[key] = done[key] + 1
             if done[key] == 4 * len(tiles):
                 width = len(tiles) * gw
+                if c == 0:
+                    half, part = divmod(tiles[0], 4)
+                    nc.scalar.copy(out=joint[half][:, part * W : part * W + BANK], in_=banks[key][:])
+                    if part:
+                        store(joint[half], 4 * half, 4, g0, gw)
+                    return
                 result = stage.tile([P, width], F32, name="result")
-                nc.scalar.copy(out=result[:], in_=banks[key][:, 0:width])
-                rows = out[tiles[0] * P : (tiles[-1] + 1) * P, g0 : g0 + gw]
-                nc.sync.dma_start(
-                    out=rows.rearrange("(u p) j -> p u j", p=P),
-                    in_=result[:].rearrange("p (u j) -> p u j", u=len(tiles)),
-                )
+                empty = nc.vector.tensor_copy if key == (3, 7) else nc.scalar.copy
+                empty(out=result[:], in_=banks[key][:, 0:width])
+                store(result, tiles[0], len(tiles), g0, gw)
 
         def own(shape, dtype, name):
             return keep.tile(shape, dtype, name=name, align_bytes=64)
@@ -337,5 +349,7 @@ def tile_list_tiert_none_kernel(
         for tiles in pairs_of_tiles[:3]:
             passes(2, tiles, ("r",))
         passes(2, pairs_of_tiles[3], (0, 1, "q", "r"))
-        for tiles in pairs_of_tiles[:3] + [(6,), (7,)]:
+        for tiles in pairs_of_tiles[:2] + [(4,), (5,), (6,)]:
             passes(3, tiles, (0, 1, "q", "r"))
+        for s in (0, HALF):
+            passes(3, (7,), (0, 1, "q", "r"), s, HALF)

@@ -293,31 +293,34 @@ def tile_list_tiert_none_kernel(
         first_tier(HALF + QUARTER, QUARTER, high)
         first_tier(0, HALF, low)
         first_tier(HALF, QUARTER, mid)
-        rounded1 = round_x(W, W, nc.scalar.copy, lent([P, PACK * W], BF16, "rounded256", 51200))
+        rounded1 = [
+            round_x(W + s, HALF, nc.scalar.copy, lent([P, PACK * HALF], BF16, "rounded%d" % (W + s), 51200 + 8 * s))
+            for s in (0, HALF)
+        ]
         for s in (0, HALF):
             left_over(s, left0)
         second_tier(0, left0, HALF)
+        first_tier(W, HALF, rounded1[0])
+        first_tier(W + HALF, HALF, rounded1[1])
         first01 = lent([P, 2 * W], U8, "first01", 20480 + MOVING_SCALES)
-        look_up_scales(0, 1, first01[:, 0:W])
-        first_tier(W, W, rounded1)
-        look_up_scales(1, 2, first01[:, W : 2 * W])
+        look_up_scales(0, 2, first01[:])
         shift_scales(0, 2, first01, nc.sync)
         load_x(2 * W, W, 32768)
         load_x(3 * W, W, 36864)
-        for tier in ("q", "r"):
-            for tiles in pairs_of_tiles:
-                passes(0, tiles, (tier,))
-
+        for tiles in pairs_of_tiles:
+            passes(0, tiles, ("q",))
         given = []
-        for s in (0, HALF):
-            deq = give_back(W + s)
-            given.append(own([P, PACK, HALF], F32, "given%d" % s))
-            nc.scalar.copy(out=given[-1][:], in_=deq[:])
+        for i, tiles in enumerate(pairs_of_tiles):
+            passes(0, tiles, ("r",))
+            if i < 2:
+                deq = give_back(W + i * HALF)
+                given.append(own([P, PACK, HALF], F32, "given%d" % i))
+                nc.scalar.copy(out=given[-1][:], in_=deq[:])
         for tiles in pairs_of_tiles:
             passes(1, tiles, ("q",))
-        look_up_words(0, lent([P, W], U32, "pairs0", 51200))
-        left1 = lent([P, PACK * W], BF16, "left1", 49664)
-        look_up_words(1, lent([P, W], U32, "pairs1", 51712), lambda: left_over(W, left1, given[0]))
+        look_up_words(0, lent([P, W], U32, "pairs0", 51712))
+        left1 = lent([P, PACK * W], BF16, "left1", 50048)
+        look_up_words(1, lent([P, W], U32, "pairs1", 52096), lambda: left_over(W, left1, given[0]))
         left_over(W + HALF, left1, given[1])
         second_tier(1, left1, HALF)
         first23 = lent([P, 2 * W], U8, "first23", 49664 + MOVING_SCALES)

@@ -21,7 +21,7 @@ W = 256
 HALF = 128
 QUARTER = 64
 NEAR = 4
-FIXED_CODES, FIXED_SCALES, MOVING_CODES, MOVING_SCALES = 0, 64, 128, 192
+FIXED_CODES, FIXED_SCALES, MOVING_CODES, MOVING_SCALES = 0, 0, 64, 192
 
 
 def tile_list_tiert_none_kernel(

from contextlib import ExitStack

import concourse.mybir as mybir

K, L, N, T, J = 1024, 512, 1024, 2048, 1024
FLOPS = 2 * N * J * (K + 2 * L)

F32 = mybir.dt.float32
BF16 = mybir.dt.bfloat16
I32 = mybir.dt.int32
U32 = mybir.dt.uint32
U16 = mybir.dt.uint16
U8 = mybir.dt.uint8
FP8X4 = mybir.dt.float8_e4m3fn_x4
FP4X4 = mybir.dt.float4_e2m1fn_x4

P = 128
PACK = 4
BANK = 512
W = 256
HALF = 128
QUARTER = 64
NEAR = 4
FIXED_CODES, FIXED_SCALES, MOVING_CODES, MOVING_SCALES = 0, 0, 64, 192


def tile_list_tiert_none_kernel(
    tc, tab_words, tab_scales, wt_words, wt_scales, x, wx_words, wx_scales, offs, out
):
    nc = tc.nc
    with ExitStack() as ctx:
        keep = ctx.enter_context(tc.tile_pool(name="keep", bufs=1))
        lend = ctx.enter_context(tc.tile_pool(name="lend", bufs=1))
        spread = ctx.enter_context(tc.tile_pool(name="spread", bufs=1))
        stage = ctx.enter_context(tc.tile_pool(name="stage", bufs=8))
        psum = ctx.enter_context(tc.psum_pool(name="psum", bufs=1))

        def bank(shape, name, b):
            return psum.tile(shape, F32, name=name, offset=2048 * b)

        taken = [4 * N]

        def operand(columns, dtype, name, phase):
            size = columns * (1 if dtype == U8 else 4)
            start = taken[-1] + phase
            taken.append((start + size + 255) // 256 * 256)
            return spread.tile([P, columns], dtype, name=name, align_bytes=64, offset=start)

        offsets = keep.tile([P, J // 16], U16, name="offsets")
        diag = lend.tile([P, 520], BF16, name="diag", align_bytes=64, offset=8192 + 448)
        tab_plane = keep.tile([P, T], U8, name="tab_plane", align_bytes=64)
        wx_plane = operand(N // 4, U8, "wx_plane", FIXED_SCALES)
        tab = keep.tile([P, T], I32, name="tab", align_bytes=64)
        wx = spread.tile([P, N], I32, name="wx", align_bytes=256, offset=0)
        wt = [operand(2 * N, U8, "wt%d" % a, FIXED_CODES) for a in range(2)]
        second = operand(J, U8, "second", MOVING_SCALES)

        wt_plane = operand(2 * N, U8, "wt_plane", FIXED_SCALES)
        nc.vector.memset(wx_plane[:].bitcast(I32), 0)
        nc.vector.memset(tab_plane[:].bitcast(I32), 0)
        nc.vector.memset(wt_plane[:].bitcast(I32), 0)
        nc.vector.memset(second[:].bitcast(I32), 0)

        nc.gpsimd.memset(diag[:].bitcast(F32), 0.0)
        nc.gpsimd.affine_select(
            out=diag[:].bitcast(F32), in_=diag[:].bitcast(F32), pattern=[[-1, 260]],
            compare_op=mybir.AluOpType.not_equal, fill=1.0, base=1, channel_multiplier=2,
        )

        raw = {}

        def load_x(j0, w, offset):
            tile = lend.tile([P, PACK, w], F32, name="raw%d" % j0, align_bytes=256, offset=offset)
            nc.sync.dma_start(out=tile[:], in_=x[:, j0 : j0 + w].rearrange("(p t) j -> p t j", t=PACK))
            for s in range(0, w, QUARTER):
                raw[j0 + s] = (tile, s)

        def load_tab_scales(r, queue):
            queue.dma_start(
                out=tab_plane[r:P:16, :].bitcast(I32),
                in_=tab_scales.rearrange("a (q r) t -> r q a t", r=4)[r].bitcast(I32),
            )

        def load_wx_scales(r, queue):
            queue.dma_start(
                out=wx_plane[32 * r : 32 * r + 16, :].bitcast(I32),
                in_=wx_scales[0, 4 * r : 4 * r + 4, :].rearrange("r (u n) -> u r n", u=4).bitcast(I32),
            )

        def load_wt_scales(r, queue):
            queue.dma_start(
                out=wt_plane[r:P:32, :].rearrange("q (a n) -> q a n", a=2).bitcast(I32),
                in_=wt_scales.rearrange("a (q r) n -> r q a n", r=4)[r].bitcast(I32),
            )

        def load_wt(a):
            nc.sync.dma_start(out=wt[a][:].bitcast(I32), in_=wt_words[a].bitcast(I32))

        load_x(0, W, 0)
        load_wx_scales(0, nc.sync)
        load_wx_scales(1, nc.sync)
        load_wx_scales(2, nc.sync)
        load_wx_scales(3, nc.sync)
        nc.sync.dma_start(out=wx[:], in_=wx_words[0].rearrange("p n b -> p (n b)").bitcast(I32))
        nc.sync.dma_start(offsets[:], offs)
        load_x(W, W, 12288)
        load_tab_scales(0, nc.sync)
        load_tab_scales(1, nc.sync)
        load_tab_scales(2, nc.sync)
        load_tab_scales(3, nc.sync)
        nc.sync.dma_start(out=tab[:], in_=tab_words[0].rearrange("p t b -> p (t b)").bitcast(I32))
        load_wt_scales(0, nc.sync)
        load_wt_scales(1, nc.sync)
        load_wt_scales(2, nc.sync)
        load_wt_scales(3, nc.sync)
        load_wt(0)
        load_wt(1)

        eye = keep.tile([P, PACK - 1, BANK], BF16, name="eye", align_bytes=64)
        eye_codes = operand(BANK, U32, "eye_codes", FIXED_CODES)
        eye_plane = operand(BANK, U8, "eye_plane", FIXED_SCALES)

        def quantise_eye(t0, t1, values):
            nc.vector.quantize_mx(
                out=eye_codes[:, t0 * P : t1 * P].bitcast(FP8X4), scales=eye_plane[:, t0 * P : t1 * P], in_=values
            )

        quantise_eye(3, 4, diag[:, 0:BANK])
        for t in range(PACK - 1):
            nc.vector.tensor_copy(out=eye[:, t, :], in_=diag[:, 3 - t : 3 - t + BANK])
        quantise_eye(0, 2, eye[:, 0:2, :].rearrange("p t c -> p (t c)"))
        quantise_eye(2, 3, eye[:, 2, :])
        spans = [(0, W), (W, W), (2 * W, W), (3 * W, W)]
        tiers = {}
        for g, (g0, gw) in enumerate(spans):
            for tier in ("q", "r"):
                tiers[(tier, g)] = (
                    lend.tile([P, W], U32, name="codes_q%d" % g, align_bytes=64, offset=(8192 + 1024, 21504)[g] + MOVING_CODES)
                    if tier == "q" and g < 2
                    else operand(gw, U32, "codes_%s%d" % (tier, g), MOVING_CODES),
                    operand(gw, U8, "plane_%s%d" % (tier, g), MOVING_SCALES),
                )

        def place(tier, j0):
            g = max(i for i, span in enumerate(spans) if span[0] <= j0)
            return tiers[(tier, g)] + (j0 - spans[g][0],)

        def woven(t):
            return t.rearrange("p (c i t) -> p c t i", i=NEAR, t=PACK)

        def planar(t):
            return t.rearrange("p t (c i) -> p c t i", i=NEAR)

        def round_x(j0, w, copy, rounded):
            tile, s = raw[j0]
            copy(out=woven(rounded[:]), in_=planar(tile[:, :, s : s + w]))
            return rounded

        def first_tier(j0, w, rounded):
            codes, plane, o = place("q", j0)
            nc.vector.quantize_mx(out=codes[:, o : o + w].bitcast(FP8X4), scales=plane[:, o : o + w], in_=rounded[:])

        def give_back(j0):
            codes, plane, o = place("q", j0)
            deq = bank([P, PACK, HALF], "deq%d" % j0, (6 if j0 < 2 * W else 0) + j0 // HALF % 2)
            for t in range(PACK):
                nc.tensor.matmul_mx(
                    out=deq[:, t, :],
                    lhsT=eye_codes[:, t * P : (t + 1) * P].bitcast(FP8X4),
                    lhsT_scale=eye_plane[:, t * P : (t + 1) * P],
                    rhs=codes[:, o : o + HALF].bitcast(FP8X4),
                    rhs_scale=plane[:, o : o + HALF],
                    start=True,
                    stop=True,
                )
            return deq

        def left_over(j0, left, deq=None):
            tile, s = raw[j0]
            deq = give_back(j0) if deq is None else deq
            nc.vector.tensor_tensor(
                out=woven(left[:, PACK * s : PACK * (s + HALF)]),
                in0=planar(tile[:, :, s : s + HALF]),
                in1=planar(deq[:]),
                op=mybir.AluOpType.subtract,
            )

        def second_tier(c, left, w=W):
            codes, plane, o = place("r", c * W)
            for s in range(0, W, w):
                nc.vector.quantize_mx(
                    out=codes[:, o + s : o + s + w].bitcast(FP8X4),
                    scales=plane[:, o + s : o + s + w],
                    in_=left[:, PACK * s : PACK * (s + w)],
                )

        planes = {}

        def look_up_scales(c0, c1, first):
            nc.vector.tensor_copy(first, tab_plane[:].indirect(offsets[:, c0 * W // 16 : c1 * W // 16]))
            for g, (g0, gw) in enumerate(spans):
                if c0 * W <= g0 < c1 * W:
                    planes[g] = (first[:, g0 - c0 * W : g0 - c0 * W + gw], second[:, g0 : g0 + gw])

        def shift_scales(c0, c1, first, queue):
            queue.dma_start(out=second[0:112, c0 * W : c1 * W].bitcast(I32), in_=first[16:P, :].bitcast(I32))

        parted = {}

        def look_up_words(c, pairs, between=None):
            g0, gw = spans[c]
            nc.vector.tensor_copy(pairs[:], tab[:].bitcast(U32).indirect(offsets[:, g0 // 16 : (g0 + gw) // 16]))
            if between is not None:
                between()
            parted[c] = operand(4 * gw, U8, "parted%d" % c, MOVING_CODES)[:].rearrange("p (a w) -> p a w", a=2)
            halves = pairs[:].bitcast(U16).rearrange("p (j d) -> p d j", d=2)
            if c == 0:
                for a in range(2):
                    nc.vector.tensor_copy(out=parted[c][:, a, :].bitcast(U16), in_=halves[:, a, :])
            else:
                nc.vector.tensor_copy(out=parted[c].bitcast(U16), in_=halves)

        banks = {}
        homes = {}
        for c, row in enumerate(((0, 1, 2, 3), (4, 5, 6, 7), (2, 3, 4, 5), (6, 7, 2, 3))):
            for i, b in enumerate(row):
                homes[(c, 2 * i)] = b
        for i, b in enumerate((0, 1, 2, 3, 4)):
            homes[(3, 4 + i)] = b
        joint = [keep.tile([P, 2 * BANK], F32, name="joint%d" % i) for i in range(2)]
        done = {}

        def store(result, m, count, g0, gw):
            nc.sync.dma_start(
                out=out[m * P : (m + count) * P, g0 : g0 + gw].rearrange("(u p) j -> p u j", p=P),
                in_=result[:].rearrange("p (u j) -> p u j", u=count),
            )

        def passes(c, tiles, kinds, s0=0, gw=W):
            key = (c, tiles[0] + s0 // HALF)
            g0 = c * W + s0
            if key not in banks:
                banks[key] = bank([P, BANK], "acc%d_%d" % key, homes[key])
                done[key] = 0
            for kind in kinds:
                for u, m in enumerate(tiles):
                    n0 = m * P
                    if kind in ("q", "r"):
                        codes, plane = tiers[(kind, c)]
                        ops = dict(
                            lhsT=wx[:, n0 : n0 + P].bitcast(FP8X4), lhsT_scale=wx_plane[4 * (m // 2) : P, (m % 2) * P : (m % 2 + 1) * P],
                            rhs=codes[:, s0 : s0 + gw].bitcast(FP8X4), rhs_scale=plane[:, s0 : s0 + gw],
                        )
                    else:
                        ops = dict(
                            lhsT=wt[kind][:, 2 * n0 : 2 * (n0 + P)].bitcast(FP4X4),
                            lhsT_scale=wt_plane[:, kind * N + n0 : kind * N + n0 + P],
                            rhs=parted[c][:, kind, 2 * s0 : 2 * (s0 + gw)].bitcast(FP4X4),
                            rhs_scale=planes[c][kind][:, s0 : s0 + gw],
                        )
                    nc.tensor.matmul_mx(
                        out=banks[key][:, u * gw : (u + 1) * gw],
                        start=(done[key] == 0),
                        stop=(done[key] == 4 * len(tiles) - 1),
                        **ops,
                    )
                    done[key] = done[key] + 1
            if done[key] == 4 * len(tiles):
                width = len(tiles) * gw
                if c == 0:
                    half, part = divmod(tiles[0], 4)
                    nc.scalar.copy(out=joint[half][:, part * W : part * W + BANK], in_=banks[key][:])
                    if part:
                        store(joint[half], 4 * half, 4, g0, gw)
                    return
                result = stage.tile([P, width], F32, name="result")
                empty = nc.vector.tensor_copy if key == (3, 7) else nc.scalar.copy
                empty(out=result[:], in_=banks[key][:, 0:width])
                store(result, tiles[0], len(tiles), g0, gw)

        def own(shape, dtype, name):
            return keep.tile(shape, dtype, name=name, align_bytes=64)

        def lent(shape, dtype, name, offset):
            return lend.tile(shape, dtype, name=name, align_bytes=64, offset=offset)

        pairs_of_tiles = [(m, m + 1) for m in range(0, N // P, 2)]

        left0 = lent([P, PACK * W], BF16, "left0", 20480)
        low = round_x(0, HALF, nc.vector.tensor_copy, lent([P, PACK * HALF], BF16, "rounded0", 8192 - 512))
        mid = round_x(HALF, QUARTER, nc.vector.tensor_copy, lent([P, PACK * QUARTER], BF16, "rounded128", 8192 + 512))
        high = round_x(HALF + QUARTER, QUARTER, nc.scalar.copy, own([P, PACK * QUARTER], BF16, "rounded192"))
        first_tier(HALF + QUARTER, QUARTER, high)
        first_tier(0, HALF, low)
        first_tier(HALF, QUARTER, mid)
        rounded1 = [
            round_x(W + s, HALF, nc.scalar.copy, lent([P, PACK * HALF], BF16, "rounded%d" % (W + s), 51200 + 8 * s))
            for s in (0, HALF)
        ]
        for s in (0, HALF):
            left_over(s, left0)
        second_tier(0, left0, HALF)
        first_tier(W, HALF, rounded1[0])
        first_tier(W + HALF, HALF, rounded1[1])
        first01 = lent([P, 2 * W], U8, "first01", 20480 + MOVING_SCALES)
        look_up_scales(0, 2, first01[:])
        shift_scales(0, 2, first01, nc.sync)
        load_x(2 * W, W, 32768)
        load_x(3 * W, W, 36864)
        for tiles in pairs_of_tiles:
            passes(0, tiles, ("q",))
        given = []
        for i, tiles in enumerate(pairs_of_tiles):
            passes(0, tiles, ("r",))
            if i < 2:
                deq = give_back(W + i * HALF)
                given.append(own([P, PACK, HALF], F32, "given%d" % i))
                nc.scalar.copy(out=given[-1][:], in_=deq[:])
        for tiles in pairs_of_tiles:
            passes(1, tiles, ("q",))
        look_up_words(0, lent([P, W], U32, "pairs0", 51712))
        left1 = lent([P, PACK * W], BF16, "left1", 50048)
        look_up_words(1, lent([P, W], U32, "pairs1", 52096), lambda: left_over(W, left1, given[0]))
        left_over(W + HALF, left1, given[1])
        second_tier(1, left1, HALF)
        first23 = lent([P, 2 * W], U8, "first23", 49664 + MOVING_SCALES)
        look_up_scales(2, 4, first23[:])
        shift_scales(2, 4, first23, nc.sync)
        first_tier(2 * W, W, round_x(2 * W, W, nc.scalar.copy, lent([P, PACK * W], BF16, "rounded512", 16384)))
        look_up_words(2, lent([P, W], U32, "pairs2", 16384))
        for a in range(2):
            for tiles in pairs_of_tiles:
                passes(0, tiles, (a,))
        for tiles in pairs_of_tiles:
            passes(1, tiles, (1, 0))
        for tiles in pairs_of_tiles:
            passes(1, tiles, ("r",))
        left2 = lent([P, PACK * W], BF16, "left2", 45056)
        left_over(2 * W, left2)
        left_over(2 * W + HALF, left2)
        second_tier(2, left2, HALF)
        first_tier(3 * W, W, round_x(3 * W, W, nc.scalar.copy, lent([P, PACK * W], BF16, "rounded768", 17408)))
        look_up_words(3, lent([P, W], U32, "pairs3", 45056))
        for kind in ("q", 0, 1):
            for tiles in pairs_of_tiles[:2]:
                passes(2, tiles, (kind,))
        passes(2, pairs_of_tiles[2], ("q", 0, 1))
        left3 = own([P, PACK * W], BF16, "left3")
        left_over(3 * W, left3)
        left_over(3 * W + HALF, left3)
        second_tier(3, left3)
        for tiles in pairs_of_tiles[:3]:
            passes(2, tiles, ("r",))
        passes(2, pairs_of_tiles[3], (0, 1, "q", "r"))
        for tiles in pairs_of_tiles[:2] + [(4,), (5,), (6,)]:
            passes(3, tiles, (0, 1, "q", "r"))
        for s in (0, HALF):
            passes(3, (7,), (0, 1, "q", "r"), s, HALF)
